import numpy as np, ml_dtypes
CORES = [2,3,42,43,82,83,122,123]
N = 8
import mx_ref
BF = ml_dtypes.bfloat16
def entries(a):
    return np.ascontiguousarray(a.T).reshape(-1)
def table(e):
    return np.ascontiguousarray(np.reshape(e, (-1, 16)).T).astype(np.int32)
def cols(t, e):
    v = np.concatenate([t.reshape(128, -1, 4), np.zeros((128, 1, 4), BF)], axis=1)
    return np.ascontiguousarray(v[:, e]).reshape(128, -1)
def f(rng, *shape):
    return mx_ref.flush((rng.standard_normal(shape, dtype=np.float32) * np.exp2(rng.integers(-2, 3, shape[:-1] + (1,)))).astype(BF))
def wide(rng, *shape, cols=0):
    v = rng.standard_normal(shape, dtype=np.float32) * np.exp2(rng.integers(-12, 13, shape)).astype(np.float32)
    if cols: v *= np.repeat(np.exp2(rng.integers(-cols, cols + 1, shape[:-2] + (1, shape[-1] // 4))) * (rng.random(shape[:-2] + (1, shape[-1] // 4)) > 0.0625), 4, axis=-1).astype(np.float32)
    return mx_ref.flush(v.astype(BF))
T, CAPP = 512, 96
def lists(rng, full=False, skew=False, single=False, back=False):
    if full:
        v = rng.permutation(([CAPP] * (T // CAPP) + [T % CAPP] + [0] * N)[:N])
        n = v[(np.arange(N)[None, :] - np.arange(N)[:, None]) % N][rng.permutation(N)][:, rng.permutation(N)]
    else:
        n = np.full((N, N), T // N)
        for _ in range(20 * N):
            (s, t), (d, e) = rng.permutation(N)[:2], rng.permutation(N)[:2]
            k = rng.integers(0, min(n[s, d], n[t, e], CAPP - n[s, e], CAPP - n[t, d]) + 1)
            n[s, d] -= k; n[t, e] -= k; n[s, e] += k; n[t, d] += k
    a = np.full((N, N * CAPP), -1)
    for s in range(N):
        parts = np.split(rng.permutation(T), np.cumsum(n[s])[:-1])
        for d in range(N): a[s, d * CAPP + rng.permutation(CAPP)[:n[s, d]]] = parts[d]
    p, u, o = [], [], []
    for r in range(N):
        used = np.flatnonzero(a[:, r * CAPP:(r + 1) * CAPP].reshape(-1) >= 0)
        p.append(table(used[::-1] if back else rng.permutation(used)))
        h = rng.integers(0, N)
        c = rng.integers(0, 2, N) if full else (np.full(N, -1) if rng.random() < 0.5 else rng.integers(0, 2, N)) if single else rng.integers(-1, 2, N)
        if c[h] < 0: c[h] = rng.integers(0, 2)
        named = np.flatnonzero(c >= 0)
        if single: named = np.array([h])
        if skew:
            m = rng.integers(T // 2 + 1, T + 1)
            e = np.sort(np.concatenate([np.full(m, h), rng.choice(named, T - m)]))
        elif full: e = np.sort(np.concatenate([named, rng.choice(named, T - N)]))
        else: e = np.repeat(named, np.diff(np.concatenate([[0], np.sort(rng.integers(0, T + 1, len(named) - 1)), [T]])))
        u.append(table(np.concatenate([c, np.full(16 - N, -1)]))); o.append(table(e))
    return {"send": np.stack([table(k) for k in a]), "place": np.stack(p), "sel": np.stack(u), "of": np.stack(o)}
def setup_inputs(rng):
    return {"x": f(rng, N, 128, 4 * T), "w": f(rng, N, 256, 512), **lists(rng)}
def setup_inputs_full(rng):
    return {**setup_inputs(rng), **lists(rng, full=True)}
def setup_inputs_reversed(rng):
    return {**setup_inputs(rng), **lists(rng, back=True)}
def setup_inputs_single(rng):
    return {**setup_inputs(rng), **lists(rng, single=True)}
def setup_inputs_skew(rng):
    return {**setup_inputs(rng), **lists(rng, skew=True)}
def setup_inputs_spread(rng):
    d = setup_inputs(rng); d["x"] = wide(rng, N, 128, 4 * T, cols=8); return d
def check_inputs(d):
    b = []
    for k in ("x", "w"):
        a = np.abs(d[k].astype(np.float32))
        if not ((a == 0) | ((a >= 2.0 ** -30) & (a <= 2.0 ** 30))).all(): b.append(k)
    sends = np.stack([entries(d["send"][r]) for r in range(N)])
    for r in range(N):
        c, p, u, e = sends[r], entries(d["place"][r]), entries(d["sel"][r]), entries(d["of"][r])
        if c.min() < -1 or not np.array_equal(np.sort(c[c >= 0]), np.arange(T)): b.append("send")
        if not np.array_equal(np.sort(p), np.flatnonzero(sends[:, r * CAPP:(r + 1) * CAPP].reshape(-1) >= 0)): b.append("place")
        if u.min() < -1 or u.max() > 1 or (u[N:] != -1).any(): b.append("sel")
        if e.min() < 0 or e.max() >= N or (np.diff(e) < 0).any() or (u[e] < 0).any(): b.append("of")
    return b
def reference(x, w, send, place, sel, of):
    W = [[mx_ref.quantize(w[h][128 * m:128 * m + 128]) for m in range(2)] for h in range(N)]
    y = np.zeros((N, 128, T), np.float32)
    for r in range(N):
        slots = np.concatenate([cols(x[s], entries(send[s])[r * CAPP:(r + 1) * CAPP]) for s in range(N)], axis=1)
        X = mx_ref.quantize(cols(slots, entries(place[r])))
        u, e = entries(sel[r]), entries(of[r])
        for h in range(N):
            i = e == h
            if i.any(): y[r][:, i] = mx_ref.matmul(W[h][u[h]], X)[:, i]
    return {"y": y}

@@ -1,0 +1,298 @@
+from concourse.bass import DstId, RemoteDMATransfer
+from concourse.mybir import dt, AluOpType, ActivationFunctionType
+
+N, CAPP, TK = 8, 96, 512
+NS = N * CAPP
+SCRATCH = {
+    "xs": ("sbuf", [128, 4 * TK], "bfloat16"),
+    "ws": ("sbuf", [128, 1024], "bfloat16"),
+    "sendl": ("sbuf", [128, 48], "int32"),
+    "soff": ("sbuf", [128, 48], "uint16"),
+    "r_c": ("sbuf", [128, NS + CAPP], "float8_e4m3fn_x4"),
+    "r_s": ("sbuf", [128, NS + CAPP], "uint8"),
+    "w_c": ("sbuf", [128, 256], "float8_e4m3fn_x4"),
+    "w_s": ("sbuf", [128, 256], "uint8"),
+    "m_c": ("sbuf", [128, 256], "float8_e4m3fn_x4"),
+    "m_s": ("sbuf", [128, 256], "uint8"),
+    "e_c": ("sbuf", [128, 768], "float8_e4m3fn_x4"),
+    "e_s": ("sbuf", [128, 768], "uint8"),
+    "ia": ("sbuf", [128, 32], "int32"),
+    "ib": ("sbuf", [128, 32], "int32"),
+    "ic": ("sbuf", [128, 32], "int32"),
+    "lin": ("sbuf", [128, 32], "float32"),
+    "selmsg": ("dram", [128, 2], "int32"),
+    "selland": ("dram", [6, 128, 2], "int32"),
+    "selr": ("sbuf", [1, 12], "int32"),
+    "selb": ("sbuf", [128, 12], "int32"),
+    "selc": ("sbuf", [128, 12], "float32"),
+    "selo": ("sbuf", [1, 16], "int32"),
+    "selq": ("sbuf", [16, 16], "int32"),
+    "selk": ("sbuf", [16, 16], "float32"),
+    "plc": ("sbuf", [16, 32], "int32"),
+    "ofl": ("sbuf", [16, 32], "int32"),
+    "f0": ("sbuf", [16, 32], "float32"),
+    "f1": ("sbuf", [16, 32], "float32"),
+    "f2": ("sbuf", [16, 32], "float32"),
+    "f3": ("sbuf", [16, 32], "float32"),
+    "f4": ("sbuf", [16, 32], "float32"),
+    "f5": ("sbuf", [16, 32], "float32"),
+    "f6": ("sbuf", [16, 32], "float32"),
+    "pu": ("sbuf", [16, 32], "uint16"),
+    "poff": ("sbuf", [128, 32], "uint16"),
+    "ps": ("psum", [128, 4096], "float32"),
+    "pw": ("sbuf", [128, 10 * NS], "float32"),
+    "yb": ("sbuf", [128, TK], "float32"),
+}
+for _k in range(4):
+    SCRATCH["tk%d" % _k] = ("sbuf", [128, 768], "bfloat16")
+for _k in range(1, 4):
+    SCRATCH["q%d_c" % _k] = ("sbuf", [128, 192], "float8_e4m3fn_x4")
+    SCRATCH["q%d_s" % _k] = ("sbuf", [128, 192], "uint8")
+    SCRATCH["et%d" % _k] = ("sbuf", [128, 1024], "bfloat16")
+    SCRATCH["eo%d" % _k] = ("sbuf", [128, 64], "uint16")
+    SCRATCH["x%d_c" % _k] = ("sbuf", [128, 256], "float8_e4m3fn_x4")
+    SCRATCH["x%d_s" % _k] = ("sbuf", [128, 256], "uint8")
+
+SEMAPHORES = (["selm", "srow", "lst", "xl", "wl", "pl", "iot", "ibs", "lns", "sos", "wq", "sela", "srr", "sbs", "scs",
+               "sqs", "sks", "sent", "me", "tok", "pus", "pr", "yg", "yh", "y0", "y1", "evAz", "evBz"]
+              + ["fs%d" % k for k in range(4)]
+              + ["tq%d" % k for k in range(4)] + ["vg%d" % k for k in range(4)] + ["sg%d" % k for k in range(4)]
+              + ["%s%d" % (s, k) for k in range(1, 4) for s in ("eos", "vge", "sge", "eq")]
+              + ["ex%d" % j for j in range(6)]
+              + ["mmA%d" % i for i in range(10)] + ["mmB%d" % i for i in range(10)]
+              + ["evA%d" % i for i in range(6)] + ["evB%d" % i for i in range(6)])
+
+
+def _groups(cores, topo):
+    out = []
+    for q in range(len(cores)):
+        for grp in out:
+            if topo.chip(cores[grp[0]]) == topo.chip(cores[q]):
+                grp.append(q)
+                break
+        else:
+            out.append([q])
+    return out
+
+
+def rank_program(g, core, T, topo):
+    r = T.rank_of(core)
+    if r is None:
+        return
+    cores = T.cores
+    groups = _groups(cores, topo)
+    C = len(groups)
+
+    def where(q):
+        return [i for i in range(C) if q in groups[i]][0]
+
+    def others(q):
+        c = where(q)
+        return [s for d in range(1, C) for s in groups[(c + d) % C]]
+
+    def shift(q):
+        return (0, CAPP * (q + 1)) if groups[where(q)][0] == q else (CAPP, CAPP * q)
+
+    def slot_col(q, s):
+        o, a = shift(q)
+        return o + (s * CAPP - a) % NS
+
+    ci = where(r)
+    mate = [q for q in groups[ci] if q != r][0]
+    first = groups[ci][0] == r
+    o, a = shift(r)
+    own0 = NS - CAPP if first else 0
+    out0 = NS if first else 0
+    oth = others(r)
+    S = T.sem
+    V, A, Te, Y = g.vector, g.scalar, g.tensor, g.sync
+    Copy = ActivationFunctionType.Copy
+    U8 = dt.uint8
+    far = cores[oth[0]]
+    eng = topo.engines(core, far)
+    lo, hi = eng[:len(eng) // 2], eng[len(eng) // 2:]
+
+    def m(es):
+        return sum(1 << e for e in es)
+
+    def dst(q):
+        ad = topo.addr(cores[q])
+        return DstId(rid=ad[0], pnc=ad[1])
+
+    sent = [0]
+
+    def pair(trs):
+        g.remote_dma_fused([RemoteDMATransfer(dst_ids=[dst(q)], dma_engine_mask=m(es), remote_sem=sem, srcs=[s], dsts=[d])
+                            for q, es, d, s, sem in trs], local_sem=S.sent)
+        sent[0] += sum(len(t[1]) for t in trs)
+
+    Y.dma_start(T.selmsg[0:8, :], T.sel[:, :]).then_inc(S.selm, 16)
+    Y.dma_start(T.selmsg[8:128, :], T["of"][0:15, 0:16]).then_inc(S.selm, 16)
+    for k in range(4):
+        Y.dma_start(T.sendl[16 * k:16 * k + 16, :], T.send[:, :]).then_inc(S.lst, 16)
+        A.dma_start(T.sendl[64 + 16 * k:80 + 16 * k, :], T.send[:, :]).then_inc(S.lst, 16)
+    A.dma_start(T.xs[:, :], T.x[:, :]).then_inc(S.xl, 16)
+    Y.dma_start(T.selo[0:1, 0:16], T.sel[:, :]).then_inc(S.srow, 16)
+    for e in range(2):
+        Y.dma_start(T.ws[:, 512 * e:512 * e + 512], T.w[128 * e:128 * e + 128, :]).then_inc(S.wl, 16)
+    Y.dma_start(T.plc[:, :], T.place[:, :]).then_inc(S.pl, 16)
+    Y.dma_start(T.ofl[:, :], T["of"][:, :]).then_inc(S.pl, 16)
+
+    g.iota(T.ia[:, :], [[0, 32]], 0, 1).then_inc(S.iot, 1)
+    g.iota(T.ic[:, :], [[16, 32]], 0, 0).then_inc(S.iot, 1)
+    g.wait_ge(S.selm, 32)
+    g.remote_dma_fused([RemoteDMATransfer(dst_ids=[dst(q) for q in oth], dma_engine_mask=m(eng[:1]), remote_sem=S.sela,
+                                          srcs=[T.selmsg[:, :]],
+                                          dsts=[T.selland[others(q).index(r)] for q in oth])], local_sem=S.sent)
+    sent[0] += 1
+    g.wait_ge(S.srow, 16)
+    g.partition_broadcast(T.selq[:, :], T.selo[:, :], 16).then_inc(S.sqs, 1)
+
+    V.wait_ge(S.iot, 2)
+    V.tensor_scalar(T.ib[:, :], T.ia[:, :], 15, None, AluOpType.bitwise_and).then_inc(S.ibs, 1)
+    V.wait_ge(S.ibs, 1)
+    V.tensor_tensor(T.lin[:, :], T.ib[:, :], T.ic[:, :], AluOpType.add).then_inc(S.lns, 1)
+    V.wait_ge(S.lst, 128)
+    V.tensor_scalar(T.soff[:, :], T.sendl[:, :], 4.0, 0.0, AluOpType.mult, AluOpType.max).then_inc(S.sos, 1)
+    V.wait_ge(S.wl, 32)
+    V.quantize_mx(T.w_c[:, :], T.w_s[:, :], T.ws[:, :]).then_inc(S.wq, 1)
+
+    ad = topo.addr(cores[mate])
+    g.wait_ge(S.wq, 1)
+    g.remote_dma(T.m_c[:, :].bitcast(U8), T.w_c[:, :].bitcast(U8), S.me, S.sent, ad[1], ad[0], m(eng))
+    g.remote_dma(T.m_s[:, :], T.w_s[:, :], S.me, S.sent, ad[1], ad[0], m(eng))
+    sent[0] += 2 * len(eng)
+
+    V.wait_ge(S.sos, 1)
+    A.wait_ge(S.sos, 1)
+    V.wait_ge(S.xl, 16)
+    A.wait_ge(S.xl, 16)
+    for k in (1, 2, 3, 0):
+        c = (ci + k) % C
+        tile = T["tk%d" % k]
+        off = T.soff[:, 12 * c:12 * c + 12]
+        for t in range(2):
+            V.tensor_copy(tile[:, t:768:4], T.xs[:, t:4 * TK].indirect(off)).then_inc(S["vg%d" % k], 1)
+        for t in range(2, 4):
+            A.activation(tile[:, t:768:4], T.xs[:, t:4 * TK].indirect(off), Copy).then_inc(S["sg%d" % k], 1)
+        V.wait_ge(S["vg%d" % k], 2)
+        V.wait_ge(S["sg%d" % k], 2)
+        if k:
+            qc, qs, b = T["q%d_c" % k], T["q%d_s" % k], 0
+        else:
+            qc, qs, b = T.r_c, T.r_s, own0
+        V.quantize_mx(qc[:, b:b + 192], qs[:, b:b + 192], tile[:, :]).then_inc(S["tq%d" % k], 1)
+        g.wait_ge(S["tq%d" % k], 1)
+        if k:
+            d1, d2 = groups[c]
+            h1, h2 = slot_col(d1, r), slot_col(d2, r)
+            pair([(d1, lo, T.r_c[:, h1:h1 + 96].bitcast(U8), qc[:, 0:96].bitcast(U8), S.tok),
+                  (d2, hi, T.r_c[:, h2:h2 + 96].bitcast(U8), qc[:, 96:192].bitcast(U8), S.tok)])
+            pair([(d1, lo, T.r_s[:, h1:h1 + 96], qs[:, 0:96], S.tok),
+                  (d2, hi, T.r_s[:, h2:h2 + 96], qs[:, 96:192], S.tok)])
+        else:
+            h1 = slot_col(mate, r)
+            g.remote_dma(T.r_c[:, h1:h1 + 96].bitcast(U8), T.r_c[:, out0:out0 + 96].bitcast(U8), S.tok, S.sent, ad[1], ad[0], m(eng))
+            g.remote_dma(T.r_s[:, h1:h1 + 96], T.r_s[:, out0:out0 + 96], S.tok, S.sent, ad[1], ad[0], m(eng))
+            sent[0] += 2 * len(eng)
+
+    Y.wait_ge(S.sela, 6)
+    Y.dma_start(T.selr[0:1, 0:12], T.selland[:, r // 2, :]).then_inc(S.srr, 16)
+    g.wait_ge(S.srr, 16)
+    g.partition_broadcast(T.selb[:, :], T.selr[:, :], 128).then_inc(S.sbs, 1)
+    V.wait_ge(S.sbs, 1)
+    V.tensor_scalar(T.selc[:, :], T.selb[:, :], 0.0, 512.0, AluOpType.max, AluOpType.mult).then_inc(S.scs, 1)
+    V.wait_ge(S.lns, 1)
+    V.wait_ge(S.scs, 1)
+    for k in range(1, 4):
+        for b in range(2):
+            j = 2 * (2 * (k - 1) + b) + r % 2
+            V.tensor_scalar(T["eo%d" % k][:, 32 * b:32 * b + 32], T.lin[:, :], T.selc[:, j:j + 1], None,
+                            AluOpType.add).then_inc(S["eos%d" % k], 1)
+    A.wait_ge(S.wl, 32)
+    SP = 40
+    for k in range(1, 4):
+        c = (ci + k) % C
+        eo, et = T["eo%d" % k], T["et%d" % k]
+        V.wait_ge(S["eos%d" % k], 2)
+        A.wait_ge(S["eos%d" % k], 2)
+        A.activation(et[:, 0:16 * SP], T.ws[:, :].indirect(eo[:, 0:SP]), Copy).then_inc(S["sge%d" % k], 1)
+        V.tensor_copy(et[:, 16 * SP:1024], T.ws[:, :].indirect(eo[:, SP:64])).then_inc(S["vge%d" % k], 1)
+        V.wait_ge(S["vge%d" % k], 1)
+        V.wait_ge(S["sge%d" % k], 1)
+        xc, xsc = T["x%d_c" % k], T["x%d_s" % k]
+        V.quantize_mx(xc[:, :], xsc[:, :], et[:, :]).then_inc(S["eq%d" % k], 1)
+        g.wait_ge(S["eq%d" % k], 1)
+        d1, d2 = groups[c]
+        j1, j2 = others(d1).index(r), others(d2).index(r)
+        pair([(d1, lo, T.e_c[:, 128 * j1:128 * j1 + 128].bitcast(U8), xc[:, 0:128].bitcast(U8), S["ex%d" % j1]),
+              (d2, hi, T.e_c[:, 128 * j2:128 * j2 + 128].bitcast(U8), xc[:, 128:256].bitcast(U8), S["ex%d" % j2])])
+        pair([(d1, lo, T.e_s[:, 128 * j1:128 * j1 + 128], xsc[:, 0:128], S["ex%d" % j1]),
+              (d2, hi, T.e_s[:, 128 * j2:128 * j2 + 128], xsc[:, 128:256], S["ex%d" % j2])])
+
+    V.wait_ge(S.sqs, 1)
+    V.tensor_scalar(T.selk[:, 0:1], T.selq[:, r:r + 1], float((8 - r) * NS), None, AluOpType.mult).then_inc(S.sks, 1)
+    V.tensor_scalar(T.selk[:, 1:2], T.selq[:, mate:mate + 1], float((9 - mate) * NS), None, AluOpType.mult).then_inc(S.sks, 1)
+    V.wait_ge(S.pl, 32)
+    V.tensor_scalar(T.f0[:, :], T.plc[:, :], float(-(a % NS)), None, AluOpType.add).then_inc(S.fs0, 1)
+    V.tensor_scalar(T.f1[:, :], T.ofl[:, :], float(NS), None, AluOpType.mult).then_inc(S.fs0, 1)
+    V.wait_ge(S.sks, 2)
+    V.tensor_scalar(T.f2[:, :], T.ofl[:, :], float(r), T.selk[:, 0:1], AluOpType.is_equal, AluOpType.mult).then_inc(S.fs0, 1)
+    V.tensor_scalar(T.f3[:, :], T.ofl[:, :], float(mate), T.selk[:, 1:2], AluOpType.is_equal, AluOpType.mult).then_inc(S.fs0, 1)
+    V.wait_ge(S.fs0, 4)
+    V.tensor_scalar(T.f4[:, :], T.f0[:, :], 0.0, float(NS), AluOpType.is_lt, AluOpType.mult).then_inc(S.fs1, 1)
+    V.tensor_tensor(T.f5[:, :], T.f2[:, :], T.f3[:, :], AluOpType.add).then_inc(S.fs1, 1)
+    V.tensor_tensor(T.f6[:, :], T.f0[:, :], T.f1[:, :], AluOpType.add).then_inc(S.fs1, 1)
+    V.wait_ge(S.fs1, 3)
+    V.tensor_tensor(T.f4[:, :], T.f4[:, :], T.f5[:, :], AluOpType.add).then_inc(S.fs2, 1)
+    V.wait_ge(S.fs2, 1)
+    V.tensor_tensor(T.f6[:, :], T.f6[:, :], T.f4[:, :], AluOpType.add).then_inc(S.fs3, 1)
+    V.wait_ge(S.fs3, 1)
+    V.tensor_copy(T.pu[:, :], T.f6[:, :]).then_inc(S.pus, 1)
+    Y.wait_ge(S.pus, 1)
+    for k in range(8):
+        Y.dma_start(T.poff[16 * k:16 * k + 16, :], T.pu[:, :]).then_inc(S.pr, 16)
+
+    blocks = [(r, T.w_c, T.w_s, 0, None, 0), (8, T.w_c, T.w_s, 128, None, 0),
+              (mate, T.m_c, T.m_s, 0, S.me, 2 * len(eng)), (9, T.m_c, T.m_s, 128, None, 0)]
+    for d in range(1, C):
+        for q in groups[(ci - d) % C]:
+            j = oth.index(q)
+            blocks.append((q, T.e_c, T.e_s, 128 * j, S["ex%d" % j], len(eng)))
+    Te.wait_ge(S.wq, 1)
+    Te.wait_ge(S.tq0, 1)
+    Te.wait_ge(S.tok, 2 * len(eng) + 6 * len(eng))
+    NB = len(blocks)
+    for i, (blk, wc, wsc, col, sem, cnt) in enumerate(blocks):
+        if sem is not None:
+            Te.wait_ge(sem, cnt)
+        if i >= 4:
+            Te.wait_ge(S["evA%d" % (i - 4)], 1)
+            Te.wait_ge(S["evB%d" % (i - 4)], 1)
+        for hf in range(2):
+            b0 = 512 * (2 * (i % 4) + hf)
+            c0 = o + 384 * hf
+            Te.matmul_mx(T.ps[:, b0:b0 + 384], wc[:, col:col + 128], wsc[:, col:col + 128],
+                         T.r_c[:, c0:c0 + 384], T.r_s[:, c0:c0 + 384], True, True).then_inc(S["mm%s%d" % ("AB"[hf], i)], 1)
+            p0 = NS * blk + 384 * hf
+            ev = S["ev%s%s" % ("AB"[hf], i if i < NB - 4 else "z")]
+            if hf == 0:
+                V.wait_ge(S["mmA%d" % i], 1)
+                V.tensor_copy(T.pw[:, p0:p0 + 384], T.ps[:, b0:b0 + 384]).then_inc(ev, 1)
+            else:
+                A.wait_ge(S["mmB%d" % i], 1)
+                A.activation(T.pw[:, p0:p0 + 384], T.ps[:, b0:b0 + 384], Copy).then_inc(ev, 1)
+
+    for E in (V, A):
+        E.wait_ge(S.pr, 128)
+        E.wait_ge(S.evAz, 4)
+        E.wait_ge(S.evBz, 4)
+    V.tensor_copy(T.yb[:, 0:256], T.pw[:, :].indirect(T.poff[:, 0:16])).then_inc(S.yg, 1)
+    A.activation(T.yb[:, 256:512], T.pw[:, :].indirect(T.poff[:, 16:32]), Copy).then_inc(S.yh, 1)
+    Y.wait_ge(S.yg, 1)
+    Y.dma_start(T.y[:, 0:256], T.yb[:, 0:256]).then_inc(S.y0, 16)
+    A.wait_ge(S.yh, 1)
+    A.dma_start(T.y[:, 256:512], T.yb[:, 256:512]).then_inc(S.y1, 16)
+    Y.wait_ge(S.y0, 16)
+    A.wait_ge(S.y1, 16)
+    g.wait_ge(S.sent, sent[0])

@@ -3,46 +3,44 @@ from concourse.mybir import dt, AluOpType, ActivationFunctionType
 
 N, CAPP, TK = 8, 96, 512
 NS = N * CAPP
+RELAYED = (1, 2)
 SCRATCH = {
     "xs": ("sbuf", [128, 4 * TK], "bfloat16"),
     "ws": ("sbuf", [128, 1024], "bfloat16"),
     "sendl": ("sbuf", [128, 48], "int32"),
     "soff": ("sbuf", [128, 48], "uint16"),
-    "r_c": ("sbuf", [128, NS + CAPP], "float8_e4m3fn_x4"),
-    "r_s": ("sbuf", [128, NS + CAPP], "uint8"),
+    "r_c": ("sbuf", [128, CAPP + NS], "float8_e4m3fn_x4"),
+    "r_s": ("sbuf", [128, CAPP + NS], "uint8"),
     "w_c": ("sbuf", [128, 256], "float8_e4m3fn_x4"),
     "w_s": ("sbuf", [128, 256], "uint8"),
     "m_c": ("sbuf", [128, 256], "float8_e4m3fn_x4"),
     "m_s": ("sbuf", [128, 256], "uint8"),
-    "e_c": ("sbuf", [128, 768], "float8_e4m3fn_x4"),
-    "e_s": ("sbuf", [128, 768], "uint8"),
+    "u_c": ("sbuf", [128, 512], "float8_e4m3fn_x4"),
+    "u_s": ("sbuf", [128, 512], "uint8"),
+    "e_c": ("sbuf", [128, 512], "float8_e4m3fn_x4"),
+    "e_s": ("sbuf", [128, 512], "uint8"),
+    "xr_c": ("sbuf", [128, 256], "float8_e4m3fn_x4"),
+    "xr_s": ("sbuf", [128, 256], "uint8"),
     "ia": ("sbuf", [128, 32], "int32"),
     "ib": ("sbuf", [128, 32], "int32"),
     "ic": ("sbuf", [128, 32], "int32"),
     "lin": ("sbuf", [128, 32], "float32"),
-    "selmsg": ("dram", [128, 2], "int32"),
-    "selland": ("dram", [6, 128, 2], "int32"),
-    "selr": ("sbuf", [1, 12], "int32"),
-    "selb": ("sbuf", [128, 12], "int32"),
-    "selc": ("sbuf", [128, 12], "float32"),
     "selo": ("sbuf", [1, 16], "int32"),
-    "selq": ("sbuf", [16, 16], "int32"),
-    "selk": ("sbuf", [16, 16], "float32"),
+    "selb": ("sbuf", [128, 16], "int32"),
+    "sland": ("sbuf", [128, 4], "int32"),
+    "selc": ("sbuf", [128, 4], "float32"),
+    "selk": ("sbuf", [16, 4], "float32"),
     "plc": ("sbuf", [16, 32], "int32"),
     "ofl": ("sbuf", [16, 32], "int32"),
-    "f0": ("sbuf", [16, 32], "float32"),
-    "f1": ("sbuf", [16, 32], "float32"),
-    "f2": ("sbuf", [16, 32], "float32"),
-    "f3": ("sbuf", [16, 32], "float32"),
-    "f4": ("sbuf", [16, 32], "float32"),
-    "f5": ("sbuf", [16, 32], "float32"),
-    "f6": ("sbuf", [16, 32], "float32"),
     "pu": ("sbuf", [16, 32], "uint16"),
     "poff": ("sbuf", [128, 32], "uint16"),
     "ps": ("psum", [128, 4096], "float32"),
-    "pw": ("sbuf", [128, 10 * NS], "float32"),
+    "pw": ("sbuf", [128, 12 * NS], "float32"),
     "yb": ("sbuf", [128, TK], "float32"),
 }
+for _k in range(12):
+    SCRATCH["i%d" % _k] = ("sbuf", [16, 32], "int32")
+    SCRATCH["f%d" % _k] = ("sbuf", [16, 32], "float32")
 for _k in range(4):
     SCRATCH["tk%d" % _k] = ("sbuf", [128, 768], "bfloat16")
 for _k in range(1, 4):
@@ -53,14 +51,14 @@ for _k in range(1, 4):
     SCRATCH["x%d_c" % _k] = ("sbuf", [128, 256], "float8_e4m3fn_x4")
     SCRATCH["x%d_s" % _k] = ("sbuf", [128, 256], "uint8")
 
-SEMAPHORES = (["selm", "srow", "lst", "xl", "wl", "pl", "iot", "ibs", "lns", "sos", "wq", "sela", "srr", "sbs", "scs",
-               "sqs", "sks", "sent", "me", "tok", "pus", "pr", "yg", "yh", "y0", "y1", "evAz", "evBz"]
-              + ["fs%d" % k for k in range(4)]
+SEMAPHORES = (["srow", "lst", "xl", "wl", "pl", "iot", "ibs", "lns", "sos", "wq", "sela", "sbs", "scs",
+               "sks", "sent", "me", "un", "us", "tokA", "tokB", "pr", "yg", "yh", "y0", "y1", "evAz", "evBz", "rec", "res"]
+              + ["fs%d" % k for k in range(9)]
               + ["tq%d" % k for k in range(4)] + ["vg%d" % k for k in range(4)] + ["sg%d" % k for k in range(4)]
-              + ["%s%d" % (s, k) for k in range(1, 4) for s in ("eos", "vge", "sge", "eq")]
-              + ["ex%d" % j for j in range(6)]
-              + ["mmA%d" % i for i in range(10)] + ["mmB%d" % i for i in range(10)]
-              + ["evA%d" % i for i in range(6)] + ["evB%d" % i for i in range(6)])
+              + ["%s%d" % (s, k) for k in range(1, 4) for s in ("eos", "vge", "sge", "eq", "rtc", "rts")]
+              + ["ex%d" % j for j in range(4)]
+              + ["mmA%d" % i for i in range(12)] + ["mmB%d" % i for i in range(12)]
+              + ["evA%d" % i for i in range(8)] + ["evB%d" % i for i in range(8)])
 
 
 def _groups(cores, topo):
@@ -75,64 +73,118 @@ def _groups(cores, topo):
     return out
 
 
+def _relay(cores, groups, q, topo):
+    able = [c for c in topo.cores_of(cores[q]) if topo.die(c) != topo.die(cores[q]) and c not in cores
+            and all(topo.may_write(c, d) for d in cores)]
+    grp = [p for p in groups if q in p][0]
+    return able[grp.index(q)]
+
+
+def _where(groups, q):
+    return [i for i in range(len(groups)) if q in groups[i]][0]
+
+
+def _others(groups, q):
+    c, n = _where(groups, q), len(groups)
+    return [s for d in range(1, n) for s in groups[(c + d) % n]]
+
+
+def _slot_col(groups, q, s):
+    d = (_where(groups, s) - _where(groups, q)) % len(groups)
+    return CAPP + CAPP * (2 * d + (s + q) % 2)
+
+
+def _pair(g, core, T, topo, sent, eng, trs):
+    half = len(eng) // 2
+    out = []
+    for i, (q, d, s, sem) in enumerate(trs):
+        ad = topo.addr(T.cores[q])
+        out.append(RemoteDMATransfer(dst_ids=[DstId(rid=ad[0], pnc=ad[1])], remote_sem=sem, srcs=[s], dsts=[d],
+                                     dma_engine_mask=sum(1 << e for e in eng[half * i:half * i + half])))
+    g.remote_dma_fused(out, local_sem=T.sem.sent)
+    sent[0] += 2 * half
+
+
+def _send_tokens(g, core, r, k, groups, T, topo, sent, eng, sems=None):
+    trs = []
+    qc, qs = T["q%d_c" % k], T["q%d_s" % k]
+    for b, d in enumerate(groups[(_where(groups, r) + k) % len(groups)]):
+        h = _slot_col(groups, d, r)
+        sem = T.sem.tokA if k == len(groups) - 1 else T.sem.tokB
+        trs.append((d, h, b, sem))
+    if sems:
+        g.wait_ge(*sems[0])
+    _pair(g, core, T, topo, sent, eng, [(d, T.r_c[:, h:h + 96].bitcast(dt.uint8), qc[:, 96 * b:96 * b + 96].bitcast(dt.uint8), sem)
+                                        for d, h, b, sem in trs])
+    if sems:
+        g.wait_ge(*sems[1])
+    _pair(g, core, T, topo, sent, eng, [(d, T.r_s[:, h:h + 96], qs[:, 96 * b:96 * b + 96], sem) for d, h, b, sem in trs])
+
+
+def _send_experts(g, core, r, k, groups, T, topo, sent, eng):
+    xc, xs = T["x%d_c" % k], T["x%d_s" % k]
+    trs = [(d, 128 * _others(groups, d).index(r), b) for b, d in enumerate(groups[(_where(groups, r) + k) % len(groups)])]
+    _pair(g, core, T, topo, sent, eng, [(d, T.e_c[:, j:j + 128].bitcast(dt.uint8), xc[:, 128 * b:128 * b + 128].bitcast(dt.uint8),
+                                         T.sem["ex%d" % (j // 128)]) for d, j, b in trs])
+    _pair(g, core, T, topo, sent, eng, [(d, T.e_s[:, j:j + 128], xs[:, 128 * b:128 * b + 128], T.sem["ex%d" % (j // 128)])
+                                        for d, j, b in trs])
+
+
+def _relay_program(g, core, r, groups, T, topo):
+    sent = [0]
+    eng = topo.engines(core, T.cores[_others(groups, r)[0]])
+    n = len(eng)
+    ci = _where(groups, r)
+    j = 128 * groups[ci].index(r)
+    to = groups[(ci + 1) % len(groups)]
+    g.wait_ge(T.sem.rec, n)
+    _pair(g, core, T, topo, sent, eng, [(d, T.u_c[:, j:j + 128].bitcast(dt.uint8), T.xr_c[:, 128 * b:128 * b + 128].bitcast(dt.uint8),
+                                         T.sem.un) for b, d in enumerate(to)])
+    g.wait_ge(T.sem.res, n)
+    _pair(g, core, T, topo, sent, eng, [(d, T.u_s[:, j:j + 128], T.xr_s[:, 128 * b:128 * b + 128], T.sem.un)
+                                        for b, d in enumerate(to)])
+    for k in RELAYED:
+        _send_tokens(g, core, r, k, groups, T, topo, sent, eng, [(T.sem["rtc%d" % k], n), (T.sem["rts%d" % k], n)])
+    g.wait_ge(T.sem.sent, sent[0])
+
+
 def rank_program(g, core, T, topo):
-    r = T.rank_of(core)
-    if r is None:
-        return
     cores = T.cores
     groups = _groups(cores, topo)
     C = len(groups)
+    r = T.rank_of(core)
+    if r is None:
+        for q in range(N):
+            if _relay(cores, groups, q, topo) == core:
+                _relay_program(g, core, q, groups, T, topo)
+        return
 
-    def where(q):
-        return [i for i in range(C) if q in groups[i]][0]
-
-    def others(q):
-        c = where(q)
-        return [s for d in range(1, C) for s in groups[(c + d) % C]]
-
-    def shift(q):
-        return (0, CAPP * (q + 1)) if groups[where(q)][0] == q else (CAPP, CAPP * q)
-
-    def slot_col(q, s):
-        o, a = shift(q)
-        return o + (s * CAPP - a) % NS
-
-    ci = where(r)
+    ci = _where(groups, r)
     mate = [q for q in groups[ci] if q != r][0]
-    first = groups[ci][0] == r
-    o, a = shift(r)
-    own0 = NS - CAPP if first else 0
-    out0 = NS if first else 0
-    oth = others(r)
+    oth = _others(groups, r)
+    prev = groups[(ci - 1) % C]
+    rel = _relay(cores, groups, r, topo)
     S = T.sem
     V, A, Te, Y = g.vector, g.scalar, g.tensor, g.sync
     Copy = ActivationFunctionType.Copy
     U8 = dt.uint8
-    far = cores[oth[0]]
-    eng = topo.engines(core, far)
-    lo, hi = eng[:len(eng) // 2], eng[len(eng) // 2:]
+    eng = topo.engines(core, cores[oth[0]])
+    ups = [e for e in topo.engines(core, cores[mate]) if e not in eng]
+    sent = [0]
 
     def m(es):
         return sum(1 << e for e in es)
 
-    def dst(q):
-        ad = topo.addr(cores[q])
-        return DstId(rid=ad[0], pnc=ad[1])
+    def chip_write(to, d, s, sem, es):
+        ad = topo.addr(to)
+        g.remote_dma(d, s, sem, S.sent, ad[1], ad[0], m(es))
+        sent[0] += len(es)
 
-    sent = [0]
-
-    def pair(trs):
-        g.remote_dma_fused([RemoteDMATransfer(dst_ids=[dst(q)], dma_engine_mask=m(es), remote_sem=sem, srcs=[s], dsts=[d])
-                            for q, es, d, s, sem in trs], local_sem=S.sent)
-        sent[0] += sum(len(t[1]) for t in trs)
-
-    Y.dma_start(T.selmsg[0:8, :], T.sel[:, :]).then_inc(S.selm, 16)
-    Y.dma_start(T.selmsg[8:128, :], T["of"][0:15, 0:16]).then_inc(S.selm, 16)
+    Y.dma_start(T.selo[0:1, 0:16], T.sel[:, :]).then_inc(S.srow, 16)
     for k in range(4):
         Y.dma_start(T.sendl[16 * k:16 * k + 16, :], T.send[:, :]).then_inc(S.lst, 16)
         A.dma_start(T.sendl[64 + 16 * k:80 + 16 * k, :], T.send[:, :]).then_inc(S.lst, 16)
     A.dma_start(T.xs[:, :], T.x[:, :]).then_inc(S.xl, 16)
-    Y.dma_start(T.selo[0:1, 0:16], T.sel[:, :]).then_inc(S.srow, 16)
     for e in range(2):
         Y.dma_start(T.ws[:, 512 * e:512 * e + 512], T.w[128 * e:128 * e + 128, :]).then_inc(S.wl, 16)
     Y.dma_start(T.plc[:, :], T.place[:, :]).then_inc(S.pl, 16)
@@ -140,13 +192,19 @@ def rank_program(g, core, T, topo):
 
     g.iota(T.ia[:, :], [[0, 32]], 0, 1).then_inc(S.iot, 1)
     g.iota(T.ic[:, :], [[16, 32]], 0, 0).then_inc(S.iot, 1)
-    g.wait_ge(S.selm, 32)
-    g.remote_dma_fused([RemoteDMATransfer(dst_ids=[dst(q) for q in oth], dma_engine_mask=m(eng[:1]), remote_sem=S.sela,
-                                          srcs=[T.selmsg[:, :]],
-                                          dsts=[T.selland[others(q).index(r)] for q in oth])], local_sem=S.sent)
-    sent[0] += 1
     g.wait_ge(S.srow, 16)
-    g.partition_broadcast(T.selq[:, :], T.selo[:, :], 16).then_inc(S.sqs, 1)
+    g.partition_broadcast(T.selb[:, :], T.selo[:, :], 128).then_inc(S.sbs, 1)
+    g.wait_ge(S.sbs, 1)
+    wants = oth[:4]
+    per = len(eng) // len(wants)
+    trs = []
+    for i, q in enumerate(wants):
+        ad = topo.addr(cores[q])
+        c = _others(groups, q).index(r) - 2
+        trs.append(RemoteDMATransfer(dst_ids=[DstId(rid=ad[0], pnc=ad[1])], dma_engine_mask=m(eng[per * i:per * i + per]),
+                                     remote_sem=S.sela, srcs=[T.selb[:, q:q + 1]], dsts=[T.sland[:, c:c + 1]]))
+    g.remote_dma_fused(trs, local_sem=S.sent)
+    sent[0] += per * len(wants)
 
     V.wait_ge(S.iot, 2)
     V.tensor_scalar(T.ib[:, :], T.ia[:, :], 15, None, AluOpType.bitwise_and).then_inc(S.ibs, 1)
@@ -157,62 +215,56 @@ def rank_program(g, core, T, topo):
     V.wait_ge(S.wl, 32)
     V.quantize_mx(T.w_c[:, :], T.w_s[:, :], T.ws[:, :]).then_inc(S.wq, 1)
 
-    ad = topo.addr(cores[mate])
     g.wait_ge(S.wq, 1)
-    g.remote_dma(T.m_c[:, :].bitcast(U8), T.w_c[:, :].bitcast(U8), S.me, S.sent, ad[1], ad[0], m(eng))
-    g.remote_dma(T.m_s[:, :], T.w_s[:, :], S.me, S.sent, ad[1], ad[0], m(eng))
-    sent[0] += 2 * len(eng)
+    chip_write(rel, T.xr_c[:, :].bitcast(U8), T.w_c[:, :].bitcast(U8), S.rec, ups)
+    chip_write(rel, T.xr_s[:, :], T.w_s[:, :], S.res, ups)
+    chip_write(cores[mate], T.m_c[:, :].bitcast(U8), T.w_c[:, :].bitcast(U8), S.me, eng)
+    chip_write(cores[mate], T.m_s[:, :], T.w_s[:, :], S.me, eng)
 
     V.wait_ge(S.sos, 1)
     A.wait_ge(S.sos, 1)
     V.wait_ge(S.xl, 16)
     A.wait_ge(S.xl, 16)
     for k in (1, 2, 3, 0):
-        c = (ci + k) % C
         tile = T["tk%d" % k]
-        off = T.soff[:, 12 * c:12 * c + 12]
+        pq = groups[(ci + k) % C] if k else [mate, r]
+        if pq[0] < pq[1]:
+            runs = [(0, 768, 6 * pq[0], 6 * pq[0] + 12)]
+        else:
+            runs = [(384 * b, 384 * b + 384, 6 * q, 6 * q + 6) for b, q in enumerate(pq)]
         for t in range(2):
-            V.tensor_copy(tile[:, t:768:4], T.xs[:, t:4 * TK].indirect(off)).then_inc(S["vg%d" % k], 1)
+            for c0, c1, l0, l1 in runs:
+                V.tensor_copy(tile[:, c0 + t:c1:4], T.xs[:, t:4 * TK].indirect(T.soff[:, l0:l1])).then_inc(S["vg%d" % k], 1)
         for t in range(2, 4):
-            A.activation(tile[:, t:768:4], T.xs[:, t:4 * TK].indirect(off), Copy).then_inc(S["sg%d" % k], 1)
-        V.wait_ge(S["vg%d" % k], 2)
-        V.wait_ge(S["sg%d" % k], 2)
-        if k:
-            qc, qs, b = T["q%d_c" % k], T["q%d_s" % k], 0
-        else:
-            qc, qs, b = T.r_c, T.r_s, own0
-        V.quantize_mx(qc[:, b:b + 192], qs[:, b:b + 192], tile[:, :]).then_inc(S["tq%d" % k], 1)
+            for c0, c1, l0, l1 in runs:
+                A.activation(tile[:, c0 + t:c1:4], T.xs[:, t:4 * TK].indirect(T.soff[:, l0:l1]), Copy).then_inc(S["sg%d" % k], 1)
+        V.wait_ge(S["vg%d" % k], 2 * len(runs))
+        V.wait_ge(S["sg%d" % k], 2 * len(runs))
+        qc, qs = (T["q%d_c" % k], T["q%d_s" % k]) if k else (T.r_c, T.r_s)
+        V.quantize_mx(qc[:, 0:192], qs[:, 0:192], tile[:, :]).then_inc(S["tq%d" % k], 1)
         g.wait_ge(S["tq%d" % k], 1)
-        if k:
-            d1, d2 = groups[c]
-            h1, h2 = slot_col(d1, r), slot_col(d2, r)
-            pair([(d1, lo, T.r_c[:, h1:h1 + 96].bitcast(U8), qc[:, 0:96].bitcast(U8), S.tok),
-                  (d2, hi, T.r_c[:, h2:h2 + 96].bitcast(U8), qc[:, 96:192].bitcast(U8), S.tok)])
-            pair([(d1, lo, T.r_s[:, h1:h1 + 96], qs[:, 0:96], S.tok),
-                  (d2, hi, T.r_s[:, h2:h2 + 96], qs[:, 96:192], S.tok)])
+        if k == 0:
+            h1 = _slot_col(groups, mate, r)
+            chip_write(cores[mate], T.r_c[:, h1:h1 + 96].bitcast(U8), T.r_c[:, 0:96].bitcast(U8), S.tokA, ups)
+            chip_write(cores[mate], T.r_s[:, h1:h1 + 96], T.r_s[:, 0:96], S.tokA, ups)
+        elif k in RELAYED:
+            chip_write(rel, qc[:, :].bitcast(U8), qc[:, :].bitcast(U8), S["rtc%d" % k], ups)
+            chip_write(rel, qs[:, :], qs[:, :], S["rts%d" % k], ups)
         else:
-            h1 = slot_col(mate, r)
-            g.remote_dma(T.r_c[:, h1:h1 + 96].bitcast(U8), T.r_c[:, out0:out0 + 96].bitcast(U8), S.tok, S.sent, ad[1], ad[0], m(eng))
-            g.remote_dma(T.r_s[:, h1:h1 + 96], T.r_s[:, out0:out0 + 96], S.tok, S.sent, ad[1], ad[0], m(eng))
-            sent[0] += 2 * len(eng)
+            _send_tokens(g, core, r, k, groups, T, topo, sent, eng)
 
-    Y.wait_ge(S.sela, 6)
-    Y.dma_start(T.selr[0:1, 0:12], T.selland[:, r // 2, :]).then_inc(S.srr, 16)
-    g.wait_ge(S.srr, 16)
-    g.partition_broadcast(T.selb[:, :], T.selr[:, :], 128).then_inc(S.sbs, 1)
-    V.wait_ge(S.sbs, 1)
-    V.tensor_scalar(T.selc[:, :], T.selb[:, :], 0.0, 512.0, AluOpType.max, AluOpType.mult).then_inc(S.scs, 1)
+    V.wait_ge(S.sela, per * len(wants))
+    V.tensor_scalar(T.selc[:, :], T.sland[:, :], 0.0, 512.0, AluOpType.max, AluOpType.mult).then_inc(S.scs, 1)
     V.wait_ge(S.lns, 1)
     V.wait_ge(S.scs, 1)
-    for k in range(1, 4):
+    for k in (2, 3):
         for b in range(2):
-            j = 2 * (2 * (k - 1) + b) + r % 2
+            j = 2 * (k - 2) + b
             V.tensor_scalar(T["eo%d" % k][:, 32 * b:32 * b + 32], T.lin[:, :], T.selc[:, j:j + 1], None,
                             AluOpType.add).then_inc(S["eos%d" % k], 1)
     A.wait_ge(S.wl, 32)
     SP = 40
-    for k in range(1, 4):
-        c = (ci + k) % C
+    for k in (2, 3):
         eo, et = T["eo%d" % k], T["et%d" % k]
         V.wait_ge(S["eos%d" % k], 2)
         A.wait_ge(S["eos%d" % k], 2)
@@ -220,68 +272,97 @@ def rank_program(g, core, T, topo):
         V.tensor_copy(et[:, 16 * SP:1024], T.ws[:, :].indirect(eo[:, SP:64])).then_inc(S["vge%d" % k], 1)
         V.wait_ge(S["vge%d" % k], 1)
         V.wait_ge(S["sge%d" % k], 1)
-        xc, xsc = T["x%d_c" % k], T["x%d_s" % k]
-        V.quantize_mx(xc[:, :], xsc[:, :], et[:, :]).then_inc(S["eq%d" % k], 1)
+        V.quantize_mx(T["x%d_c" % k][:, :], T["x%d_s" % k][:, :], et[:, :]).then_inc(S["eq%d" % k], 1)
         g.wait_ge(S["eq%d" % k], 1)
-        d1, d2 = groups[c]
-        j1, j2 = others(d1).index(r), others(d2).index(r)
-        pair([(d1, lo, T.e_c[:, 128 * j1:128 * j1 + 128].bitcast(U8), xc[:, 0:128].bitcast(U8), S["ex%d" % j1]),
-              (d2, hi, T.e_c[:, 128 * j2:128 * j2 + 128].bitcast(U8), xc[:, 128:256].bitcast(U8), S["ex%d" % j2])])
-        pair([(d1, lo, T.e_s[:, 128 * j1:128 * j1 + 128], xsc[:, 0:128], S["ex%d" % j1]),
-              (d2, hi, T.e_s[:, 128 * j2:128 * j2 + 128], xsc[:, 128:256], S["ex%d" % j2])])
+        _send_experts(g, core, r, k, groups, T, topo, sent, eng)
 
-    V.wait_ge(S.sqs, 1)
-    V.tensor_scalar(T.selk[:, 0:1], T.selq[:, r:r + 1], float((8 - r) * NS), None, AluOpType.mult).then_inc(S.sks, 1)
-    V.tensor_scalar(T.selk[:, 1:2], T.selq[:, mate:mate + 1], float((9 - mate) * NS), None, AluOpType.mult).then_inc(S.sks, 1)
+    g.wait_ge(S.un, 2 * len(eng))
+    chip_write(cores[mate], T.u_c[:, 256:512].bitcast(U8), T.u_c[:, 0:256].bitcast(U8), S.us, ups)
+    chip_write(cores[mate], T.u_s[:, 256:512], T.u_s[:, 0:256], S.us, ups)
+
+    add, mul = AluOpType.add, AluOpType.mult
+    both = [(r, 8), (mate, 9), (prev[0], 10), (prev[1], 11)]
+    V.wait_ge(S.sbs, 1)
+    for i, (q, b) in enumerate(both):
+        V.tensor_scalar(T.selk[:, i:i + 1], T.selb[0:16, q:q + 1], float((b - q) * NS), None, mul).then_inc(S.sks, 1)
     V.wait_ge(S.pl, 32)
-    V.tensor_scalar(T.f0[:, :], T.plc[:, :], float(-(a % NS)), None, AluOpType.add).then_inc(S.fs0, 1)
-    V.tensor_scalar(T.f1[:, :], T.ofl[:, :], float(NS), None, AluOpType.mult).then_inc(S.fs0, 1)
-    V.wait_ge(S.sks, 2)
-    V.tensor_scalar(T.f2[:, :], T.ofl[:, :], float(r), T.selk[:, 0:1], AluOpType.is_equal, AluOpType.mult).then_inc(S.fs0, 1)
-    V.tensor_scalar(T.f3[:, :], T.ofl[:, :], float(mate), T.selk[:, 1:2], AluOpType.is_equal, AluOpType.mult).then_inc(S.fs0, 1)
-    V.wait_ge(S.fs0, 4)
-    V.tensor_scalar(T.f4[:, :], T.f0[:, :], 0.0, float(NS), AluOpType.is_lt, AluOpType.mult).then_inc(S.fs1, 1)
-    V.tensor_tensor(T.f5[:, :], T.f2[:, :], T.f3[:, :], AluOpType.add).then_inc(S.fs1, 1)
-    V.tensor_tensor(T.f6[:, :], T.f0[:, :], T.f1[:, :], AluOpType.add).then_inc(S.fs1, 1)
+    V.tensor_scalar(T.i0[:, :], T.plc[:, :], 683.0, None, mul).then_inc(S.fs0, 1)
+    V.tensor_scalar(T.f1[:, :], T.ofl[:, :], float(NS), None, mul).then_inc(S.fs0, 1)
+    V.wait_ge(S.sks, 4)
+    for i, (q, b) in enumerate(both):
+        V.tensor_scalar(T["f%d" % (8 + i)][:, :], T.ofl[:, :], float(q), T.selk[:, i:i + 1],
+                        AluOpType.is_equal, mul).then_inc(S.fs0, 1)
+    V.wait_ge(S.fs0, 6)
+    V.tensor_scalar(T.i1[:, :], T.i0[:, :], 16, None, AluOpType.arith_shift_right).then_inc(S.fs1, 1)
+    V.tensor_tensor(T.f2[:, :], T.f8[:, :], T.f9[:, :], add).then_inc(S.fs1, 1)
+    V.tensor_tensor(T.f3[:, :], T.f10[:, :], T.f11[:, :], add).then_inc(S.fs1, 1)
     V.wait_ge(S.fs1, 3)
-    V.tensor_tensor(T.f4[:, :], T.f4[:, :], T.f5[:, :], AluOpType.add).then_inc(S.fs2, 1)
-    V.wait_ge(S.fs2, 1)
-    V.tensor_tensor(T.f6[:, :], T.f6[:, :], T.f4[:, :], AluOpType.add).then_inc(S.fs3, 1)
-    V.wait_ge(S.fs3, 1)
-    V.tensor_copy(T.pu[:, :], T.f6[:, :]).then_inc(S.pus, 1)
-    Y.wait_ge(S.pus, 1)
+    V.tensor_scalar(T.i2[:, :], T.i1[:, :], float(-2 * ci), None, add).then_inc(S.fs2, 1)
+    V.tensor_scalar(T.i3[:, :], T.i1[:, :], float(r), None, add).then_inc(S.fs2, 1)
+    V.tensor_tensor(T.f5[:, :], T.f2[:, :], T.f1[:, :], add).then_inc(S.fs2, 1)
+    V.tensor_tensor(T.f4[:, :], T.f3[:, :], T.plc[:, :], add).then_inc(S.fs2, 1)
+    V.wait_ge(S.fs2, 4)
+    V.tensor_scalar(T.i4[:, :], T.i2[:, :], 6, None, AluOpType.bitwise_and).then_inc(S.fs3, 1)
+    V.tensor_scalar(T.i5[:, :], T.i3[:, :], 1, None, AluOpType.bitwise_and).then_inc(S.fs3, 1)
+    V.tensor_tensor(T.f6[:, :], T.f5[:, :], T.f4[:, :], add).then_inc(S.fs3, 1)
+    V.wait_ge(S.fs3, 3)
+    V.tensor_tensor(T.i6[:, :], T.i4[:, :], T.i5[:, :], add).then_inc(S.fs4, 1)
+    V.wait_ge(S.fs4, 1)
+    V.tensor_tensor(T.i7[:, :], T.i6[:, :], T.i1[:, :], AluOpType.subtract).then_inc(S.fs5, 1)
+    V.wait_ge(S.fs5, 1)
+    V.tensor_scalar(T.f7[:, :], T.i7[:, :], float(CAPP), None, mul).then_inc(S.fs6, 1)
+    V.wait_ge(S.fs6, 1)
+    V.tensor_tensor(T.f0[:, :], T.f7[:, :], T.f6[:, :], add).then_inc(S.fs7, 1)
+    V.wait_ge(S.fs7, 1)
+    V.tensor_copy(T.pu[:, :], T.f0[:, :]).then_inc(S.fs8, 1)
+    Y.wait_ge(S.fs8, 1)
     for k in range(8):
         Y.dma_start(T.poff[16 * k:16 * k + 16, :], T.pu[:, :]).then_inc(S.pr, 16)
 
     blocks = [(r, T.w_c, T.w_s, 0, None, 0), (8, T.w_c, T.w_s, 128, None, 0),
               (mate, T.m_c, T.m_s, 0, S.me, 2 * len(eng)), (9, T.m_c, T.m_s, 128, None, 0)]
-    for d in range(1, C):
-        for q in groups[(ci - d) % C]:
-            j = oth.index(q)
-            blocks.append((q, T.e_c, T.e_s, 128 * j, S["ex%d" % j], len(eng)))
-    Te.wait_ge(S.wq, 1)
-    Te.wait_ge(S.tq0, 1)
-    Te.wait_ge(S.tok, 2 * len(eng) + 6 * len(eng))
+    mine = groups[ci].index(r)
+    for q, b in both[2:]:
+        blocks.append((b if mine else q, T.u_c, T.u_s, 128 * prev.index(q), S.un, 2 * len(eng)))
+    for q in groups[(ci - 2) % C]:
+        blocks.append((q, T.e_c, T.e_s, 128 * oth.index(q), S["ex%d" % oth.index(q)], len(eng)))
+    for q, b in both[2:]:
+        blocks.append((q if mine else b, T.u_c, T.u_s, 256 + 128 * prev.index(q), S.us, 2 * len(ups)))
+    for q in groups[(ci - 3) % C]:
+        blocks.append((q, T.e_c, T.e_s, 128 * oth.index(q), S["ex%d" % oth.index(q)], len(eng)))
     NB = len(blocks)
-    for i, (blk, wc, wsc, col, sem, cnt) in enumerate(blocks):
-        if sem is not None:
+
+    def product(i, hf):
+        blk, wc, wsc, col, sem, cnt = blocks[i]
+        if sem is not None and hf == 0:
             Te.wait_ge(sem, cnt)
-        if i >= 4:
+        if i >= 4 and hf == 0:
             Te.wait_ge(S["evA%d" % (i - 4)], 1)
             Te.wait_ge(S["evB%d" % (i - 4)], 1)
-        for hf in range(2):
-            b0 = 512 * (2 * (i % 4) + hf)
-            c0 = o + 384 * hf
-            Te.matmul_mx(T.ps[:, b0:b0 + 384], wc[:, col:col + 128], wsc[:, col:col + 128],
-                         T.r_c[:, c0:c0 + 384], T.r_s[:, c0:c0 + 384], True, True).then_inc(S["mm%s%d" % ("AB"[hf], i)], 1)
-            p0 = NS * blk + 384 * hf
-            ev = S["ev%s%s" % ("AB"[hf], i if i < NB - 4 else "z")]
-            if hf == 0:
-                V.wait_ge(S["mmA%d" % i], 1)
-                V.tensor_copy(T.pw[:, p0:p0 + 384], T.ps[:, b0:b0 + 384]).then_inc(ev, 1)
-            else:
-                A.wait_ge(S["mmB%d" % i], 1)
-                A.activation(T.pw[:, p0:p0 + 384], T.ps[:, b0:b0 + 384], Copy).then_inc(ev, 1)
+        b0 = 512 * (2 * (i % 4) + hf)
+        c0 = CAPP + 384 * hf
+        Te.matmul_mx(T.ps[:, b0:b0 + 384], wc[:, col:col + 128], wsc[:, col:col + 128],
+                     T.r_c[:, c0:c0 + 384], T.r_s[:, c0:c0 + 384], True, True).then_inc(S["mm%s%d" % ("AB"[hf], i)], 1)
+        p0 = NS * blk + 384 * hf
+        ev = S["ev%s%s" % ("AB"[hf], i if i < NB - 4 else "z")]
+        if hf == 0:
+            V.wait_ge(S["mmA%d" % i], 1)
+            V.tensor_copy(T.pw[:, p0:p0 + 384], T.ps[:, b0:b0 + 384]).then_inc(ev, 1)
+        else:
+            A.wait_ge(S["mmB%d" % i], 1)
+            A.activation(T.pw[:, p0:p0 + 384], T.ps[:, b0:b0 + 384], Copy).then_inc(ev, 1)
+
+    Te.wait_ge(S.wq, 1)
+    Te.wait_ge(S.tq0, 1)
+    Te.wait_ge(S.tokA, 2 * len(ups) + 2 * len(eng))
+    for i in range(4):
+        product(i, 0)
+    Te.wait_ge(S.tokB, 4 * len(eng))
+    for i in range(4):
+        product(i, 1)
+    for i in range(4, NB):
+        product(i, 0)
+        product(i, 1)
 
     for E in (V, A):
         E.wait_ge(S.pr, 128)

@@ -3,7 +3,10 @@ from concourse.mybir import dt, AluOpType, ActivationFunctionType
 
 N, CAPP, TK = 8, 96, 512
 NS = N * CAPP
-RELAYED = (1, 2)
+HALF = NS // 2
+SP = 40
+TORD = (1, 3, 2)
+EORD = (3, 2)
 SCRATCH = {
     "xs": ("sbuf", [128, 4 * TK], "bfloat16"),
     "ws": ("sbuf", [128, 1024], "bfloat16"),
@@ -26,10 +29,10 @@ SCRATCH = {
     "ic": ("sbuf", [128, 32], "int32"),
     "lin": ("sbuf", [128, 32], "float32"),
     "selo": ("sbuf", [1, 16], "int32"),
-    "selb": ("sbuf", [128, 16], "int32"),
-    "sland": ("sbuf", [128, 4], "int32"),
-    "selc": ("sbuf", [128, 4], "float32"),
-    "selk": ("sbuf", [16, 4], "float32"),
+    "self5": ("sbuf", [1, 16], "float32"),
+    "selb": ("sbuf", [128, 16], "float32"),
+    "sland": ("sbuf", [128, 4], "float32"),
+    "selk": ("sbuf", [16, 8], "float32"),
     "plc": ("sbuf", [16, 32], "int32"),
     "ofl": ("sbuf", [16, 32], "int32"),
     "pu": ("sbuf", [16, 32], "uint16"),
@@ -38,27 +41,26 @@ SCRATCH = {
     "pw": ("sbuf", [128, 12 * NS], "float32"),
     "yb": ("sbuf", [128, TK], "float32"),
 }
-for _k in range(12):
-    SCRATCH["i%d" % _k] = ("sbuf", [16, 32], "int32")
+for _k in range(14):
     SCRATCH["f%d" % _k] = ("sbuf", [16, 32], "float32")
 for _k in range(4):
     SCRATCH["tk%d" % _k] = ("sbuf", [128, 768], "bfloat16")
 for _k in range(1, 4):
     SCRATCH["q%d_c" % _k] = ("sbuf", [128, 192], "float8_e4m3fn_x4")
     SCRATCH["q%d_s" % _k] = ("sbuf", [128, 192], "uint8")
+for _k in (2, 3):
     SCRATCH["et%d" % _k] = ("sbuf", [128, 1024], "bfloat16")
     SCRATCH["eo%d" % _k] = ("sbuf", [128, 64], "uint16")
     SCRATCH["x%d_c" % _k] = ("sbuf", [128, 256], "float8_e4m3fn_x4")
     SCRATCH["x%d_s" % _k] = ("sbuf", [128, 256], "uint8")
 
-SEMAPHORES = (["srow", "lst", "xl", "wl", "pl", "iot", "ibs", "lns", "sos", "wq", "sela", "sbs", "scs",
-               "sks", "sent", "me", "un", "us", "tokA", "tokB", "pr", "yg", "yh", "y0", "y1", "evAz", "evBz", "rec", "res"]
-              + ["fs%d" % k for k in range(9)]
-              + ["tq%d" % k for k in range(4)] + ["vg%d" % k for k in range(4)] + ["sg%d" % k for k in range(4)]
-              + ["%s%d" % (s, k) for k in range(1, 4) for s in ("eos", "vge", "sge", "eq", "rtc", "rts")]
+SEMAPHORES = (["srow", "lst", "xl", "wl", "pl", "iot", "ibs", "lns", "scs", "sbs", "sos", "wq", "sela", "sks", "sent",
+               "me", "un", "us", "tokM", "pr", "yg", "yh", "y0", "y1", "rec", "res", "evz"]
+              + ["fs%d" % k for k in range(5)] + ["tok%d" % k for k in range(1, 4)]
+              + ["%s%d" % (s, k) for k in range(4) for s in ("tq", "vg", "sg")]
+              + ["%s%d" % (s, k) for k in (2, 3) for s in ("eos", "vge", "sge", "eq", "rec", "res")]
               + ["ex%d" % j for j in range(4)]
-              + ["mmA%d" % i for i in range(12)] + ["mmB%d" % i for i in range(12)]
-              + ["evA%d" % i for i in range(8)] + ["evB%d" % i for i in range(8)])
+              + ["mm%d" % i for i in range(24)] + ["ev%d" % i for i in range(16)])
 
 
 def _groups(cores, topo):
@@ -73,15 +75,14 @@ def _groups(cores, topo):
     return out
 
 
+def _where(groups, q):
+    return [i for i in range(len(groups)) if q in groups[i]][0]
+
+
 def _relay(cores, groups, q, topo):
     able = [c for c in topo.cores_of(cores[q]) if topo.die(c) != topo.die(cores[q]) and c not in cores
             and all(topo.may_write(c, d) for d in cores)]
-    grp = [p for p in groups if q in p][0]
-    return able[grp.index(q)]
-
-
-def _where(groups, q):
-    return [i for i in range(len(groups)) if q in groups[i]][0]
+    return able[groups[_where(groups, q)].index(q)]
 
 
 def _others(groups, q):
@@ -89,12 +90,29 @@ def _others(groups, q):
     return [s for d in range(1, n) for s in groups[(c + d) % n]]
 
 
+def _base(groups, q):
+    c = _where(groups, q)
+    return (c - groups[c].index(q)) % len(groups)
+
+
+def _half_col(groups, q, hf):
+    second = groups[_where(groups, q)].index(q)
+    return hf * (HALF + CAPP) if second else CAPP + hf * HALF
+
+
 def _slot_col(groups, q, s):
-    d = (_where(groups, s) - _where(groups, q)) % len(groups)
-    return CAPP + CAPP * (2 * d + (s + q) % 2)
+    c = _where(groups, s)
+    p = CAPP * (2 * ((c - _base(groups, q)) % len(groups)) + groups[c].index(s))
+    return _half_col(groups, q, p // HALF) + p % HALF
 
 
-def _pair(g, core, T, topo, sent, eng, trs):
+def _write(g, T, topo, sent, es, to, d, s, sem):
+    ad = topo.addr(to)
+    g.remote_dma(d, s, sem, T.sem.sent, ad[1], ad[0], sum(1 << e for e in es))
+    sent[0] += len(es)
+
+
+def _pair(g, T, topo, sent, eng, trs):
     half = len(eng) // 2
     out = []
     for i, (q, d, s, sem) in enumerate(trs):
@@ -105,46 +123,35 @@ def _pair(g, core, T, topo, sent, eng, trs):
     sent[0] += 2 * half
 
 
-def _send_tokens(g, core, r, k, groups, T, topo, sent, eng, sems=None):
-    trs = []
-    qc, qs = T["q%d_c" % k], T["q%d_s" % k]
-    for b, d in enumerate(groups[(_where(groups, r) + k) % len(groups)]):
-        h = _slot_col(groups, d, r)
-        sem = T.sem.tokA if k == len(groups) - 1 else T.sem.tokB
-        trs.append((d, h, b, sem))
-    if sems:
-        g.wait_ge(*sems[0])
-    _pair(g, core, T, topo, sent, eng, [(d, T.r_c[:, h:h + 96].bitcast(dt.uint8), qc[:, 96 * b:96 * b + 96].bitcast(dt.uint8), sem)
-                                        for d, h, b, sem in trs])
-    if sems:
-        g.wait_ge(*sems[1])
-    _pair(g, core, T, topo, sent, eng, [(d, T.r_s[:, h:h + 96], qs[:, 96 * b:96 * b + 96], sem) for d, h, b, sem in trs])
-
-
-def _send_experts(g, core, r, k, groups, T, topo, sent, eng):
-    xc, xs = T["x%d_c" % k], T["x%d_s" % k]
-    trs = [(d, 128 * _others(groups, d).index(r), b) for b, d in enumerate(groups[(_where(groups, r) + k) % len(groups)])]
-    _pair(g, core, T, topo, sent, eng, [(d, T.e_c[:, j:j + 128].bitcast(dt.uint8), xc[:, 128 * b:128 * b + 128].bitcast(dt.uint8),
-                                         T.sem["ex%d" % (j // 128)]) for d, j, b in trs])
-    _pair(g, core, T, topo, sent, eng, [(d, T.e_s[:, j:j + 128], xs[:, 128 * b:128 * b + 128], T.sem["ex%d" % (j // 128)])
-                                        for d, j, b in trs])
+def _chosen(g, r, k, b, plane, groups, T, topo, sent, eng):
+    d = groups[(_where(groups, r) + k) % len(groups)][b]
+    j = _others(groups, d).index(r)
+    sem = T.sem["ex%d" % j]
+    if plane:
+        _write(g, T, topo, sent, eng, T.cores[d], T.e_s[:, 128 * j:128 * j + 128],
+               T["x%d_s" % k][:, 128 * b:128 * b + 128], sem)
+    else:
+        _write(g, T, topo, sent, eng, T.cores[d], T.e_c[:, 128 * j:128 * j + 128].bitcast(dt.uint8),
+               T["x%d_c" % k][:, 128 * b:128 * b + 128].bitcast(dt.uint8), sem)
 
 
 def _relay_program(g, core, r, groups, T, topo):
     sent = [0]
     eng = topo.engines(core, T.cores[_others(groups, r)[0]])
-    n = len(eng)
+    ups = [e for e in topo.engines(core, T.cores[r]) if e not in eng]
     ci = _where(groups, r)
     j = 128 * groups[ci].index(r)
     to = groups[(ci + 1) % len(groups)]
-    g.wait_ge(T.sem.rec, n)
-    _pair(g, core, T, topo, sent, eng, [(d, T.u_c[:, j:j + 128].bitcast(dt.uint8), T.xr_c[:, 128 * b:128 * b + 128].bitcast(dt.uint8),
-                                         T.sem.un) for b, d in enumerate(to)])
-    g.wait_ge(T.sem.res, n)
-    _pair(g, core, T, topo, sent, eng, [(d, T.u_s[:, j:j + 128], T.xr_s[:, 128 * b:128 * b + 128], T.sem.un)
-                                        for b, d in enumerate(to)])
-    for k in RELAYED:
-        _send_tokens(g, core, r, k, groups, T, topo, sent, eng, [(T.sem["rtc%d" % k], n), (T.sem["rts%d" % k], n)])
+    g.wait_ge(T.sem.rec, len(ups))
+    _pair(g, T, topo, sent, eng, [(d, T.u_c[:, j:j + 128].bitcast(dt.uint8), T.xr_c[:, 128 * b:128 * b + 128].bitcast(dt.uint8),
+                                   T.sem.un) for b, d in enumerate(to)])
+    g.wait_ge(T.sem.res, len(ups))
+    _pair(g, T, topo, sent, eng, [(d, T.u_s[:, j:j + 128], T.xr_s[:, 128 * b:128 * b + 128], T.sem.un) for b, d in enumerate(to)])
+    for k in EORD:
+        g.wait_ge(T.sem["rec%d" % k], len(ups))
+        _chosen(g, r, k, 1, False, groups, T, topo, sent, eng)
+        g.wait_ge(T.sem["res%d" % k], len(ups))
+        _chosen(g, r, k, 1, True, groups, T, topo, sent, eng)
     g.wait_ge(T.sem.sent, sent[0])
 
 
@@ -160,6 +167,7 @@ def rank_program(g, core, T, topo):
         return
 
     ci = _where(groups, r)
+    mine = groups[ci].index(r)
     mate = [q for q in groups[ci] if q != r][0]
     oth = _others(groups, r)
     prev = groups[(ci - 1) % C]
@@ -168,32 +176,34 @@ def rank_program(g, core, T, topo):
     V, A, Te, Y = g.vector, g.scalar, g.tensor, g.sync
     Copy = ActivationFunctionType.Copy
     U8 = dt.uint8
+    add, mul = AluOpType.add, AluOpType.mult
     eng = topo.engines(core, cores[oth[0]])
     ups = [e for e in topo.engines(core, cores[mate]) if e not in eng]
     sent = [0]
 
-    def m(es):
-        return sum(1 << e for e in es)
-
-    def chip_write(to, d, s, sem, es):
-        ad = topo.addr(to)
-        g.remote_dma(d, s, sem, S.sent, ad[1], ad[0], m(es))
-        sent[0] += len(es)
+    def chip_write(to, d, s, sem):
+        _write(g, T, topo, sent, ups, to, d, s, sem)
 
     Y.dma_start(T.selo[0:1, 0:16], T.sel[:, :]).then_inc(S.srow, 16)
+    A.dma_start(T.plc[:, :], T.place[:, :]).then_inc(S.pl, 16)
+    A.dma_start(T.ofl[:, :], T["of"][:, :]).then_inc(S.pl, 16)
     for k in range(4):
         Y.dma_start(T.sendl[16 * k:16 * k + 16, :], T.send[:, :]).then_inc(S.lst, 16)
         A.dma_start(T.sendl[64 + 16 * k:80 + 16 * k, :], T.send[:, :]).then_inc(S.lst, 16)
-    A.dma_start(T.xs[:, :], T.x[:, :]).then_inc(S.xl, 16)
     for e in range(2):
         Y.dma_start(T.ws[:, 512 * e:512 * e + 512], T.w[128 * e:128 * e + 128, :]).then_inc(S.wl, 16)
-    Y.dma_start(T.plc[:, :], T.place[:, :]).then_inc(S.pl, 16)
-    Y.dma_start(T.ofl[:, :], T["of"][:, :]).then_inc(S.pl, 16)
+    A.dma_start(T.xs[:, :], T.x[:, :]).then_inc(S.xl, 16)
 
     g.iota(T.ia[:, :], [[0, 32]], 0, 1).then_inc(S.iot, 1)
     g.iota(T.ic[:, :], [[16, 32]], 0, 0).then_inc(S.iot, 1)
-    g.wait_ge(S.srow, 16)
-    g.partition_broadcast(T.selb[:, :], T.selo[:, :], 128).then_inc(S.sbs, 1)
+    V.wait_ge(S.iot, 2)
+    V.tensor_scalar(T.ib[:, :], T.ia[:, :], 15, None, AluOpType.bitwise_and).then_inc(S.ibs, 1)
+    V.wait_ge(S.ibs, 1)
+    V.tensor_tensor(T.lin[:, :], T.ib[:, :], T.ic[:, :], add).then_inc(S.lns, 1)
+    V.wait_ge(S.srow, 16)
+    V.tensor_scalar(T.self5[:, :], T.selo[:, :], 512.0, None, mul).then_inc(S.scs, 1)
+    g.wait_ge(S.scs, 1)
+    g.partition_broadcast(T.selb[:, :], T.self5[:, :], 128).then_inc(S.sbs, 1)
     g.wait_ge(S.sbs, 1)
     wants = oth[:4]
     per = len(eng) // len(wants)
@@ -201,173 +211,185 @@ def rank_program(g, core, T, topo):
     for i, q in enumerate(wants):
         ad = topo.addr(cores[q])
         c = _others(groups, q).index(r) - 2
-        trs.append(RemoteDMATransfer(dst_ids=[DstId(rid=ad[0], pnc=ad[1])], dma_engine_mask=m(eng[per * i:per * i + per]),
-                                     remote_sem=S.sela, srcs=[T.selb[:, q:q + 1]], dsts=[T.sland[:, c:c + 1]]))
+        trs.append(RemoteDMATransfer(dst_ids=[DstId(rid=ad[0], pnc=ad[1])], remote_sem=S.sela,
+                                     dma_engine_mask=sum(1 << e for e in eng[per * i:per * i + per]),
+                                     srcs=[T.selb[:, q:q + 1]], dsts=[T.sland[:, c:c + 1]]))
     g.remote_dma_fused(trs, local_sem=S.sent)
     sent[0] += per * len(wants)
 
-    V.wait_ge(S.iot, 2)
-    V.tensor_scalar(T.ib[:, :], T.ia[:, :], 15, None, AluOpType.bitwise_and).then_inc(S.ibs, 1)
-    V.wait_ge(S.ibs, 1)
-    V.tensor_tensor(T.lin[:, :], T.ib[:, :], T.ic[:, :], AluOpType.add).then_inc(S.lns, 1)
     V.wait_ge(S.lst, 128)
-    V.tensor_scalar(T.soff[:, :], T.sendl[:, :], 4.0, 0.0, AluOpType.mult, AluOpType.max).then_inc(S.sos, 1)
+    V.tensor_scalar(T.soff[:, :], T.sendl[:, :], 4.0, 0.0, mul, AluOpType.max).then_inc(S.sos, 1)
+
+    first = prev[0]
+    rot = 2 * CAPP * _base(groups, r)
+    both = prev + groups[ci]
+
+    def block(q, e=0):
+        return (q - first) % N + N * e
+
+    V.wait_ge(S.pl, 32)
+    terms, nf = [T.plc], [0]
+
+    def term(src, *a):
+        o = T["f%d" % nf[0]]
+        nf[0] += 1
+        V.tensor_scalar(o[:, :], src[:, :], *a).then_inc(S.fs0, 1)
+        terms.append(o)
+
+    term(T.ofl, float(NS), float(-rot - NS * first), mul, add)
+    if rot:
+        term(T.plc, float(rot), float(NS), AluOpType.is_lt, mul)
+    if first:
+        term(T.ofl, float(first), float(N * NS), AluOpType.is_lt, mul)
+    V.wait_ge(S.sbs, 1)
+    V.tensor_scalar(T.selk[:, :], T.selb[0:16, 0:8], float(N * NS // 512), None, mul).then_inc(S.sks, 1)
+    V.wait_ge(S.sks, 1)
+    for q in both:
+        term(T.ofl, float(q), T.selk[:, q:q + 1], AluOpType.is_equal, mul)
+    V.wait_ge(S.fs0, len(terms) - 1)
+    lvl = 1
+    while len(terms) > 1:
+        new = []
+        for i in range(0, len(terms) - 1, 2):
+            o = T["f%d" % nf[0]]
+            nf[0] += 1
+            V.tensor_tensor(o[:, :], terms[i][:, :], terms[i + 1][:, :], add).then_inc(S["fs%d" % lvl], 1)
+            new.append(o)
+        V.wait_ge(S["fs%d" % lvl], len(new))
+        terms = new + terms[2 * len(new):]
+        lvl += 1
+    V.tensor_copy(T.pu[:, :], terms[0][:, :]).then_inc(S.fs4, 1)
+    Y.wait_ge(S.fs4, 1)
+    for k in range(8):
+        Y.dma_start(T.poff[16 * k:16 * k + 16, :], T.pu[:, :]).then_inc(S.pr, 16)
+
     V.wait_ge(S.wl, 32)
     V.quantize_mx(T.w_c[:, :], T.w_s[:, :], T.ws[:, :]).then_inc(S.wq, 1)
-
     g.wait_ge(S.wq, 1)
-    chip_write(rel, T.xr_c[:, :].bitcast(U8), T.w_c[:, :].bitcast(U8), S.rec, ups)
-    chip_write(rel, T.xr_s[:, :], T.w_s[:, :], S.res, ups)
-    chip_write(cores[mate], T.m_c[:, :].bitcast(U8), T.w_c[:, :].bitcast(U8), S.me, eng)
-    chip_write(cores[mate], T.m_s[:, :], T.w_s[:, :], S.me, eng)
+    chip_write(rel, T.xr_c[:, :].bitcast(U8), T.w_c[:, :].bitcast(U8), S.rec)
+    chip_write(rel, T.xr_s[:, :], T.w_s[:, :], S.res)
 
     V.wait_ge(S.sos, 1)
     A.wait_ge(S.sos, 1)
     V.wait_ge(S.xl, 16)
     A.wait_ge(S.xl, 16)
-    for k in (1, 2, 3, 0):
+
+    def tokens(k, nv):
         tile = T["tk%d" % k]
-        pq = groups[(ci + k) % C] if k else [mate, r]
-        if pq[0] < pq[1]:
-            runs = [(0, 768, 6 * pq[0], 6 * pq[0] + 12)]
+        if k:
+            q = groups[(ci + k) % C][0]
+            runs = [(0, 768, 6 * q, 6 * q + 12)]
         else:
-            runs = [(384 * b, 384 * b + 384, 6 * q, 6 * q + 6) for b, q in enumerate(pq)]
-        for t in range(2):
+            runs = [(384 * b, 384 * b + 384, 6 * q, 6 * q + 6) for b, q in enumerate([r, mate] if mine else [mate, r])]
+        for t in range(4):
             for c0, c1, l0, l1 in runs:
-                V.tensor_copy(tile[:, c0 + t:c1:4], T.xs[:, t:4 * TK].indirect(T.soff[:, l0:l1])).then_inc(S["vg%d" % k], 1)
-        for t in range(2, 4):
-            for c0, c1, l0, l1 in runs:
-                A.activation(tile[:, c0 + t:c1:4], T.xs[:, t:4 * TK].indirect(T.soff[:, l0:l1]), Copy).then_inc(S["sg%d" % k], 1)
-        V.wait_ge(S["vg%d" % k], 2 * len(runs))
-        V.wait_ge(S["sg%d" % k], 2 * len(runs))
-        qc, qs = (T["q%d_c" % k], T["q%d_s" % k]) if k else (T.r_c, T.r_s)
-        V.quantize_mx(qc[:, 0:192], qs[:, 0:192], tile[:, :]).then_inc(S["tq%d" % k], 1)
+                win = T.xs[:, t:4 * TK].indirect(T.soff[:, l0:l1])
+                if t < nv:
+                    V.tensor_copy(tile[:, c0 + t:c1:4], win).then_inc(S["vg%d" % k], 1)
+                else:
+                    A.activation(tile[:, c0 + t:c1:4], win, Copy).then_inc(S["sg%d" % k], 1)
+        if nv:
+            V.wait_ge(S["vg%d" % k], nv * len(runs))
+        V.wait_ge(S["sg%d" % k], (4 - nv) * len(runs))
+        qc, qs, c = (T["q%d_c" % k], T["q%d_s" % k], 0) if k else (T.r_c, T.r_s, 3 * CAPP * mine)
+        V.quantize_mx(qc[:, c:c + 192], qs[:, c:c + 192], tile[:, :]).then_inc(S["tq%d" % k], 1)
         g.wait_ge(S["tq%d" % k], 1)
         if k == 0:
-            h1 = _slot_col(groups, mate, r)
-            chip_write(cores[mate], T.r_c[:, h1:h1 + 96].bitcast(U8), T.r_c[:, 0:96].bitcast(U8), S.tokA, ups)
-            chip_write(cores[mate], T.r_s[:, h1:h1 + 96], T.r_s[:, 0:96], S.tokA, ups)
-        elif k in RELAYED:
-            chip_write(rel, qc[:, :].bitcast(U8), qc[:, :].bitcast(U8), S["rtc%d" % k], ups)
-            chip_write(rel, qs[:, :], qs[:, :], S["rts%d" % k], ups)
-        else:
-            _send_tokens(g, core, r, k, groups, T, topo, sent, eng)
+            c, h = 4 * CAPP * mine, _slot_col(groups, mate, r)
+            chip_write(cores[mate], T.r_c[:, h:h + 96].bitcast(U8), T.r_c[:, c:c + 96].bitcast(U8), S.tokM)
+            chip_write(cores[mate], T.r_s[:, h:h + 96], T.r_s[:, c:c + 96], S.tokM)
+            return
+        to = [(d, _slot_col(groups, d, r), 96 * b) for b, d in enumerate(groups[(ci + k) % C])]
+        sem = S["tok%d" % k]
+        _pair(g, T, topo, sent, eng, [(d, T.r_c[:, h:h + 96].bitcast(U8), qc[:, b:b + 96].bitcast(U8), sem) for d, h, b in to])
+        _pair(g, T, topo, sent, eng, [(d, T.r_s[:, h:h + 96], qs[:, b:b + 96], sem) for d, h, b in to])
+
+    tokens(TORD[0], 2)
+    chip_write(cores[mate], T.m_c[:, :].bitcast(U8), T.w_c[:, :].bitcast(U8), S.me)
+    chip_write(cores[mate], T.m_s[:, :], T.w_s[:, :], S.me)
+    tokens(TORD[1], 2)
+    tokens(TORD[2], 2)
 
     V.wait_ge(S.sela, per * len(wants))
-    V.tensor_scalar(T.selc[:, :], T.sland[:, :], 0.0, 512.0, AluOpType.max, AluOpType.mult).then_inc(S.scs, 1)
     V.wait_ge(S.lns, 1)
-    V.wait_ge(S.scs, 1)
-    for k in (2, 3):
+    for k in EORD:
         for b in range(2):
             j = 2 * (k - 2) + b
-            V.tensor_scalar(T["eo%d" % k][:, 32 * b:32 * b + 32], T.lin[:, :], T.selc[:, j:j + 1], None,
-                            AluOpType.add).then_inc(S["eos%d" % k], 1)
+            V.tensor_scalar(T["eo%d" % k][:, 32 * b:32 * b + 32], T.lin[:, :], T.sland[:, j:j + 1], 0.0,
+                            add, AluOpType.max).then_inc(S["eos%d" % k], 1)
+    tokens(0, 0)
     A.wait_ge(S.wl, 32)
-    SP = 40
-    for k in (2, 3):
+    for k in EORD:
         eo, et = T["eo%d" % k], T["et%d" % k]
+        xc, xp = T["x%d_c" % k], T["x%d_s" % k]
         V.wait_ge(S["eos%d" % k], 2)
         A.wait_ge(S["eos%d" % k], 2)
         A.activation(et[:, 0:16 * SP], T.ws[:, :].indirect(eo[:, 0:SP]), Copy).then_inc(S["sge%d" % k], 1)
         V.tensor_copy(et[:, 16 * SP:1024], T.ws[:, :].indirect(eo[:, SP:64])).then_inc(S["vge%d" % k], 1)
         V.wait_ge(S["vge%d" % k], 1)
         V.wait_ge(S["sge%d" % k], 1)
-        V.quantize_mx(T["x%d_c" % k][:, :], T["x%d_s" % k][:, :], et[:, :]).then_inc(S["eq%d" % k], 1)
+        V.quantize_mx(xc[:, :], xp[:, :], et[:, :]).then_inc(S["eq%d" % k], 1)
         g.wait_ge(S["eq%d" % k], 1)
-        _send_experts(g, core, r, k, groups, T, topo, sent, eng)
+        chip_write(rel, xc[:, 128:256].bitcast(U8), xc[:, 128:256].bitcast(U8), S["rec%d" % k])
+        chip_write(rel, xp[:, 128:256], xp[:, 128:256], S["res%d" % k])
+        _chosen(g, r, k, 0, False, groups, T, topo, sent, eng)
+        _chosen(g, r, k, 0, True, groups, T, topo, sent, eng)
 
     g.wait_ge(S.un, 2 * len(eng))
-    chip_write(cores[mate], T.u_c[:, 256:512].bitcast(U8), T.u_c[:, 0:256].bitcast(U8), S.us, ups)
-    chip_write(cores[mate], T.u_s[:, 256:512], T.u_s[:, 0:256], S.us, ups)
+    chip_write(cores[mate], T.u_c[:, 256:512].bitcast(U8), T.u_c[:, 0:256].bitcast(U8), S.us)
+    chip_write(cores[mate], T.u_s[:, 256:512], T.u_s[:, 0:256], S.us)
 
-    add, mul = AluOpType.add, AluOpType.mult
-    both = [(r, 8), (mate, 9), (prev[0], 10), (prev[1], 11)]
-    V.wait_ge(S.sbs, 1)
-    for i, (q, b) in enumerate(both):
-        V.tensor_scalar(T.selk[:, i:i + 1], T.selb[0:16, q:q + 1], float((b - q) * NS), None, mul).then_inc(S.sks, 1)
-    V.wait_ge(S.pl, 32)
-    V.tensor_scalar(T.i0[:, :], T.plc[:, :], 683.0, None, mul).then_inc(S.fs0, 1)
-    V.tensor_scalar(T.f1[:, :], T.ofl[:, :], float(NS), None, mul).then_inc(S.fs0, 1)
-    V.wait_ge(S.sks, 4)
-    for i, (q, b) in enumerate(both):
-        V.tensor_scalar(T["f%d" % (8 + i)][:, :], T.ofl[:, :], float(q), T.selk[:, i:i + 1],
-                        AluOpType.is_equal, mul).then_inc(S.fs0, 1)
-    V.wait_ge(S.fs0, 6)
-    V.tensor_scalar(T.i1[:, :], T.i0[:, :], 16, None, AluOpType.arith_shift_right).then_inc(S.fs1, 1)
-    V.tensor_tensor(T.f2[:, :], T.f8[:, :], T.f9[:, :], add).then_inc(S.fs1, 1)
-    V.tensor_tensor(T.f3[:, :], T.f10[:, :], T.f11[:, :], add).then_inc(S.fs1, 1)
-    V.wait_ge(S.fs1, 3)
-    V.tensor_scalar(T.i2[:, :], T.i1[:, :], float(-2 * ci), None, add).then_inc(S.fs2, 1)
-    V.tensor_scalar(T.i3[:, :], T.i1[:, :], float(r), None, add).then_inc(S.fs2, 1)
-    V.tensor_tensor(T.f5[:, :], T.f2[:, :], T.f1[:, :], add).then_inc(S.fs2, 1)
-    V.tensor_tensor(T.f4[:, :], T.f3[:, :], T.plc[:, :], add).then_inc(S.fs2, 1)
-    V.wait_ge(S.fs2, 4)
-    V.tensor_scalar(T.i4[:, :], T.i2[:, :], 6, None, AluOpType.bitwise_and).then_inc(S.fs3, 1)
-    V.tensor_scalar(T.i5[:, :], T.i3[:, :], 1, None, AluOpType.bitwise_and).then_inc(S.fs3, 1)
-    V.tensor_tensor(T.f6[:, :], T.f5[:, :], T.f4[:, :], add).then_inc(S.fs3, 1)
-    V.wait_ge(S.fs3, 3)
-    V.tensor_tensor(T.i6[:, :], T.i4[:, :], T.i5[:, :], add).then_inc(S.fs4, 1)
-    V.wait_ge(S.fs4, 1)
-    V.tensor_tensor(T.i7[:, :], T.i6[:, :], T.i1[:, :], AluOpType.subtract).then_inc(S.fs5, 1)
-    V.wait_ge(S.fs5, 1)
-    V.tensor_scalar(T.f7[:, :], T.i7[:, :], float(CAPP), None, mul).then_inc(S.fs6, 1)
-    V.wait_ge(S.fs6, 1)
-    V.tensor_tensor(T.f0[:, :], T.f7[:, :], T.f6[:, :], add).then_inc(S.fs7, 1)
-    V.wait_ge(S.fs7, 1)
-    V.tensor_copy(T.pu[:, :], T.f0[:, :]).then_inc(S.fs8, 1)
-    Y.wait_ge(S.fs8, 1)
-    for k in range(8):
-        Y.dma_start(T.poff[16 * k:16 * k + 16, :], T.pu[:, :]).then_inc(S.pr, 16)
+    blocks = [(block(r), T.w_c, T.w_s, 0, S.wq, 1), (block(r, 1), T.w_c, T.w_s, 128, None, 0),
+              (block(mate), T.m_c, T.m_s, 0, S.me, 2 * len(ups)), (block(mate, 1), T.m_c, T.m_s, 128, None, 0)]
 
-    blocks = [(r, T.w_c, T.w_s, 0, None, 0), (8, T.w_c, T.w_s, 128, None, 0),
-              (mate, T.m_c, T.m_s, 0, S.me, 2 * len(eng)), (9, T.m_c, T.m_s, 128, None, 0)]
-    mine = groups[ci].index(r)
-    for q, b in both[2:]:
-        blocks.append((b if mine else q, T.u_c, T.u_s, 128 * prev.index(q), S.un, 2 * len(eng)))
-    for q in groups[(ci - 2) % C]:
-        blocks.append((q, T.e_c, T.e_s, 128 * oth.index(q), S["ex%d" % oth.index(q)], len(eng)))
-    for q, b in both[2:]:
-        blocks.append((q if mine else b, T.u_c, T.u_s, 256 + 128 * prev.index(q), S.us, 2 * len(ups)))
-    for q in groups[(ci - 3) % C]:
-        blocks.append((q, T.e_c, T.e_s, 128 * oth.index(q), S["ex%d" % oth.index(q)], len(eng)))
-    NB = len(blocks)
+    def chosen(k):
+        for q in groups[(ci - k) % C]:
+            j = oth.index(q)
+            blocks.append((block(q), T.e_c, T.e_s, 128 * j, S["ex%d" % j], 2 * len(eng)))
 
-    def product(i, hf):
-        blk, wc, wsc, col, sem, cnt = blocks[i]
-        if sem is not None and hf == 0:
+    for i, q in enumerate(prev):
+        blocks.append((block(q, mine), T.u_c, T.u_s, 128 * i, S.un, 2 * len(eng)))
+    chosen(EORD[0])
+    for i, q in enumerate(prev):
+        blocks.append((block(q, 1 - mine), T.u_c, T.u_s, 256 + 128 * i, S.us, 2 * len(ups)))
+    chosen(EORD[1])
+
+    half_chips = [[(_base(groups, r) + 2 * hf + j) % C for j in range(2)] for hf in range(2)]
+    h0 = [hf for hf in range(2) if (ci - TORD[-1]) % C not in half_chips[hf]][0]
+    units = ([(i, h0) for i in range(4)] + [(i, 1 - h0) for i in range(4)]
+             + [(i, hf) for i in range(4, len(blocks)) for hf in (h0, 1 - h0)])
+    waited = set()
+
+    def once(sem, cnt):
+        if sem is not None and sem not in waited:
+            waited.add(sem)
             Te.wait_ge(sem, cnt)
-        if i >= 4 and hf == 0:
-            Te.wait_ge(S["evA%d" % (i - 4)], 1)
-            Te.wait_ge(S["evB%d" % (i - 4)], 1)
-        b0 = 512 * (2 * (i % 4) + hf)
-        c0 = CAPP + 384 * hf
-        Te.matmul_mx(T.ps[:, b0:b0 + 384], wc[:, col:col + 128], wsc[:, col:col + 128],
-                     T.r_c[:, c0:c0 + 384], T.r_s[:, c0:c0 + 384], True, True).then_inc(S["mm%s%d" % ("AB"[hf], i)], 1)
-        p0 = NS * blk + 384 * hf
-        ev = S["ev%s%s" % ("AB"[hf], i if i < NB - 4 else "z")]
-        if hf == 0:
-            V.wait_ge(S["mmA%d" % i], 1)
-            V.tensor_copy(T.pw[:, p0:p0 + 384], T.ps[:, b0:b0 + 384]).then_inc(ev, 1)
-        else:
-            A.wait_ge(S["mmB%d" % i], 1)
-            A.activation(T.pw[:, p0:p0 + 384], T.ps[:, b0:b0 + 384], Copy).then_inc(ev, 1)
 
-    Te.wait_ge(S.wq, 1)
-    Te.wait_ge(S.tq0, 1)
-    Te.wait_ge(S.tokA, 2 * len(ups) + 2 * len(eng))
-    for i in range(4):
-        product(i, 0)
-    Te.wait_ge(S.tokB, 4 * len(eng))
-    for i in range(4):
-        product(i, 1)
-    for i in range(4, NB):
-        product(i, 0)
-        product(i, 1)
+    for u, (i, hf) in enumerate(units):
+        blk, wc, wsc, col, sem, cnt = blocks[i]
+        once(sem, cnt)
+        for c in half_chips[hf]:
+            if c == ci:
+                once(S.tq0, 1)
+                once(S.tokM, 2 * len(ups))
+            else:
+                once(S["tok%d" % ((ci - c) % C)], 2 * len(eng))
+        if u >= 8:
+            Te.wait_ge(S["ev%d" % (u - 8)], 1)
+        b0, c0, p0 = 512 * (u % 8), _half_col(groups, r, hf), NS * blk + HALF * hf
+        Te.matmul_mx(T.ps[:, b0:b0 + HALF], wc[:, col:col + 128], wsc[:, col:col + 128],
+                     T.r_c[:, c0:c0 + HALF], T.r_s[:, c0:c0 + HALF], True, True).then_inc(S["mm%d" % u], 1)
+        ev = S["ev%d" % u] if u < len(units) - 8 else S.evz
+        if u % 2 == 0:
+            V.wait_ge(S["mm%d" % u], 1)
+            V.tensor_copy(T.pw[:, p0:p0 + HALF], T.ps[:, b0:b0 + HALF]).then_inc(ev, 1)
+        else:
+            A.wait_ge(S["mm%d" % u], 1)
+            A.activation(T.pw[:, p0:p0 + HALF], T.ps[:, b0:b0 + HALF], Copy).then_inc(ev, 1)
 
     for E in (V, A):
         E.wait_ge(S.pr, 128)
-        E.wait_ge(S.evAz, 4)
-        E.wait_ge(S.evBz, 4)
+        E.wait_ge(S.evz, 8)
     V.tensor_copy(T.yb[:, 0:256], T.pw[:, :].indirect(T.poff[:, 0:16])).then_inc(S.yg, 1)
     A.activation(T.yb[:, 256:512], T.pw[:, :].indirect(T.poff[:, 16:32]), Copy).then_inc(S.yh, 1)
     Y.wait_ge(S.yg, 1)

from concourse.bass import DstId, RemoteDMATransfer
from concourse.mybir import dt, AluOpType, ActivationFunctionType

N, CAPP, TK = 8, 96, 512
NS = N * CAPP
HALF = NS // 2
SP = 40
TORD = (1, 3, 2)
EORD = (3, 2)
SCRATCH = {
    "xs": ("sbuf", [128, 4 * TK], "bfloat16"),
    "ws": ("sbuf", [128, 1024], "bfloat16"),
    "sendl": ("sbuf", [128, 48], "int32"),
    "soff": ("sbuf", [128, 48], "uint16"),
    "r_c": ("sbuf", [128, CAPP + NS], "float8_e4m3fn_x4"),
    "r_s": ("sbuf", [128, CAPP + NS], "uint8"),
    "w_c": ("sbuf", [128, 256], "float8_e4m3fn_x4"),
    "w_s": ("sbuf", [128, 256], "uint8"),
    "m_c": ("sbuf", [128, 256], "float8_e4m3fn_x4"),
    "m_s": ("sbuf", [128, 256], "uint8"),
    "u_c": ("sbuf", [128, 512], "float8_e4m3fn_x4"),
    "u_s": ("sbuf", [128, 512], "uint8"),
    "e_c": ("sbuf", [128, 512], "float8_e4m3fn_x4"),
    "e_s": ("sbuf", [128, 512], "uint8"),
    "xr_c": ("sbuf", [128, 256], "float8_e4m3fn_x4"),
    "xr_s": ("sbuf", [128, 256], "uint8"),
    "ia": ("sbuf", [128, 32], "int32"),
    "ib": ("sbuf", [128, 32], "int32"),
    "ic": ("sbuf", [128, 32], "int32"),
    "lin": ("sbuf", [128, 32], "float32"),
    "selo": ("sbuf", [1, 16], "int32"),
    "self5": ("sbuf", [1, 16], "float32"),
    "selb": ("sbuf", [128, 16], "float32"),
    "sland": ("sbuf", [128, 4], "float32"),
    "selk": ("sbuf", [16, 8], "float32"),
    "plc": ("sbuf", [16, 32], "int32"),
    "ofl": ("sbuf", [16, 32], "int32"),
    "pu": ("sbuf", [16, 32], "uint16"),
    "poff": ("sbuf", [128, 32], "uint16"),
    "ps": ("psum", [128, 4096], "float32"),
    "pw": ("sbuf", [128, 12 * NS], "float32"),
    "yb": ("sbuf", [128, TK], "float32"),
}
for _k in range(14):
    SCRATCH["f%d" % _k] = ("sbuf", [16, 32], "float32")
for _k in range(4):
    SCRATCH["tk%d" % _k] = ("sbuf", [128, 768], "bfloat16")
for _k in range(1, 4):
    SCRATCH["q%d_c" % _k] = ("sbuf", [128, 192], "float8_e4m3fn_x4")
    SCRATCH["q%d_s" % _k] = ("sbuf", [128, 192], "uint8")
for _k in (2, 3):
    SCRATCH["et%d" % _k] = ("sbuf", [128, 1024], "bfloat16")
    SCRATCH["eo%d" % _k] = ("sbuf", [128, 64], "uint16")
    SCRATCH["x%d_c" % _k] = ("sbuf", [128, 256], "float8_e4m3fn_x4")
    SCRATCH["x%d_s" % _k] = ("sbuf", [128, 256], "uint8")

SEMAPHORES = (["srow", "lst", "xl", "wl", "pl", "iot", "ibs", "lns", "scs", "sbs", "sos", "wq", "sela", "sks", "sent",
               "me", "un", "us", "tokM", "pr", "yg", "yh", "y0", "y1", "rec", "res", "evz"]
              + ["fs%d" % k for k in range(5)] + ["tok%d" % k for k in range(1, 4)]
              + ["%s%d" % (s, k) for k in range(4) for s in ("tq", "vg", "sg")]
              + ["%s%d" % (s, k) for k in (2, 3) for s in ("eos", "vge", "sge", "eq", "rec", "res")]
              + ["ex%d" % j for j in range(4)]
              + ["mm%d" % i for i in range(24)] + ["ev%d" % i for i in range(16)])


def _groups(cores, topo):
    out = []
    for q in range(len(cores)):
        for grp in out:
            if topo.chip(cores[grp[0]]) == topo.chip(cores[q]):
                grp.append(q)
                break
        else:
            out.append([q])
    return out


def _where(groups, q):
    return [i for i in range(len(groups)) if q in groups[i]][0]


def _relay(cores, groups, q, topo):
    able = [c for c in topo.cores_of(cores[q]) if topo.die(c) != topo.die(cores[q]) and c not in cores
            and all(topo.may_write(c, d) for d in cores)]
    return able[groups[_where(groups, q)].index(q)]


def _others(groups, q):
    c, n = _where(groups, q), len(groups)
    return [s for d in range(1, n) for s in groups[(c + d) % n]]


def _base(groups, q):
    c = _where(groups, q)
    return (c - groups[c].index(q)) % len(groups)


def _half_col(groups, q, hf):
    second = groups[_where(groups, q)].index(q)
    return hf * (HALF + CAPP) if second else CAPP + hf * HALF


def _slot_col(groups, q, s):
    c = _where(groups, s)
    p = CAPP * (2 * ((c - _base(groups, q)) % len(groups)) + groups[c].index(s))
    return _half_col(groups, q, p // HALF) + p % HALF


def _write(g, T, topo, sent, es, to, d, s, sem):
    ad = topo.addr(to)
    g.remote_dma(d, s, sem, T.sem.sent, ad[1], ad[0], sum(1 << e for e in es))
    sent[0] += len(es)


def _pair(g, T, topo, sent, eng, trs):
    half = len(eng) // 2
    out = []
    for i, (q, d, s, sem) in enumerate(trs):
        ad = topo.addr(T.cores[q])
        out.append(RemoteDMATransfer(dst_ids=[DstId(rid=ad[0], pnc=ad[1])], remote_sem=sem, srcs=[s], dsts=[d],
                                     dma_engine_mask=sum(1 << e for e in eng[half * i:half * i + half])))
    g.remote_dma_fused(out, local_sem=T.sem.sent)
    sent[0] += 2 * half


def _chosen(g, r, k, b, plane, groups, T, topo, sent, eng):
    d = groups[(_where(groups, r) + k) % len(groups)][b]
    j = _others(groups, d).index(r)
    sem = T.sem["ex%d" % j]
    if plane:
        _write(g, T, topo, sent, eng, T.cores[d], T.e_s[:, 128 * j:128 * j + 128],
               T["x%d_s" % k][:, 128 * b:128 * b + 128], sem)
    else:
        _write(g, T, topo, sent, eng, T.cores[d], T.e_c[:, 128 * j:128 * j + 128].bitcast(dt.uint8),
               T["x%d_c" % k][:, 128 * b:128 * b + 128].bitcast(dt.uint8), sem)


def _relay_program(g, core, r, groups, T, topo):
    sent = [0]
    eng = topo.engines(core, T.cores[_others(groups, r)[0]])
    ups = [e for e in topo.engines(core, T.cores[r]) if e not in eng]
    ci = _where(groups, r)
    j = 128 * groups[ci].index(r)
    to = groups[(ci + 1) % len(groups)]
    g.wait_ge(T.sem.rec, len(ups))
    _pair(g, T, topo, sent, eng, [(d, T.u_c[:, j:j + 128].bitcast(dt.uint8), T.xr_c[:, 128 * b:128 * b + 128].bitcast(dt.uint8),
                                   T.sem.un) for b, d in enumerate(to)])
    g.wait_ge(T.sem.res, len(ups))
    _pair(g, T, topo, sent, eng, [(d, T.u_s[:, j:j + 128], T.xr_s[:, 128 * b:128 * b + 128], T.sem.un) for b, d in enumerate(to)])
    for k in EORD:
        g.wait_ge(T.sem["rec%d" % k], len(ups))
        _chosen(g, r, k, 1, False, groups, T, topo, sent, eng)
        g.wait_ge(T.sem["res%d" % k], len(ups))
        _chosen(g, r, k, 1, True, groups, T, topo, sent, eng)
    g.wait_ge(T.sem.sent, sent[0])


def rank_program(g, core, T, topo):
    cores = T.cores
    groups = _groups(cores, topo)
    C = len(groups)
    r = T.rank_of(core)
    if r is None:
        for q in range(N):
            if _relay(cores, groups, q, topo) == core:
                _relay_program(g, core, q, groups, T, topo)
        return

    ci = _where(groups, r)
    mine = groups[ci].index(r)
    mate = [q for q in groups[ci] if q != r][0]
    oth = _others(groups, r)
    prev = groups[(ci - 1) % C]
    rel = _relay(cores, groups, r, topo)
    S = T.sem
    V, A, Te, Y = g.vector, g.scalar, g.tensor, g.sync
    Copy = ActivationFunctionType.Copy
    U8 = dt.uint8
    add, mul = AluOpType.add, AluOpType.mult
    eng = topo.engines(core, cores[oth[0]])
    ups = [e for e in topo.engines(core, cores[mate]) if e not in eng]
    sent = [0]

    def chip_write(to, d, s, sem):
        _write(g, T, topo, sent, ups, to, d, s, sem)

    Y.dma_start(T.selo[0:1, 0:16], T.sel[:, :]).then_inc(S.srow, 16)
    A.dma_start(T.plc[:, :], T.place[:, :]).then_inc(S.pl, 16)
    A.dma_start(T.ofl[:, :], T["of"][:, :]).then_inc(S.pl, 16)
    for k in range(4):
        Y.dma_start(T.sendl[16 * k:16 * k + 16, :], T.send[:, :]).then_inc(S.lst, 16)
        A.dma_start(T.sendl[64 + 16 * k:80 + 16 * k, :], T.send[:, :]).then_inc(S.lst, 16)
    for e in range(2):
        Y.dma_start(T.ws[:, 512 * e:512 * e + 512], T.w[128 * e:128 * e + 128, :]).then_inc(S.wl, 16)
    A.dma_start(T.xs[:, :], T.x[:, :]).then_inc(S.xl, 16)

    g.iota(T.ia[:, :], [[0, 32]], 0, 1).then_inc(S.iot, 1)
    g.iota(T.ic[:, :], [[16, 32]], 0, 0).then_inc(S.iot, 1)
    V.wait_ge(S.iot, 2)
    V.tensor_scalar(T.ib[:, :], T.ia[:, :], 15, None, AluOpType.bitwise_and).then_inc(S.ibs, 1)
    V.wait_ge(S.ibs, 1)
    V.tensor_tensor(T.lin[:, :], T.ib[:, :], T.ic[:, :], add).then_inc(S.lns, 1)
    V.wait_ge(S.srow, 16)
    V.tensor_scalar(T.self5[:, :], T.selo[:, :], 512.0, None, mul).then_inc(S.scs, 1)
    g.wait_ge(S.scs, 1)
    g.partition_broadcast(T.selb[:, :], T.self5[:, :], 128).then_inc(S.sbs, 1)
    g.wait_ge(S.sbs, 1)
    wants = oth[:4]
    per = len(eng) // len(wants)
    trs = []
    for i, q in enumerate(wants):
        ad = topo.addr(cores[q])
        c = _others(groups, q).index(r) - 2
        trs.append(RemoteDMATransfer(dst_ids=[DstId(rid=ad[0], pnc=ad[1])], remote_sem=S.sela,
                                     dma_engine_mask=sum(1 << e for e in eng[per * i:per * i + per]),
                                     srcs=[T.selb[:, q:q + 1]], dsts=[T.sland[:, c:c + 1]]))
    g.remote_dma_fused(trs, local_sem=S.sent)
    sent[0] += per * len(wants)

    V.wait_ge(S.lst, 128)
    V.tensor_scalar(T.soff[:, :], T.sendl[:, :], 4.0, 0.0, mul, AluOpType.max).then_inc(S.sos, 1)

    first = prev[0]
    rot = 2 * CAPP * _base(groups, r)
    both = prev + groups[ci]

    def block(q, e=0):
        return (q - first) % N + N * e

    V.wait_ge(S.pl, 32)
    terms, nf = [T.plc], [0]

    def term(src, *a):
        o = T["f%d" % nf[0]]
        nf[0] += 1
        V.tensor_scalar(o[:, :], src[:, :], *a).then_inc(S.fs0, 1)
        terms.append(o)

    term(T.ofl, float(NS), float(-rot - NS * first), mul, add)
    if rot:
        term(T.plc, float(rot), float(NS), AluOpType.is_lt, mul)
    if first:
        term(T.ofl, float(first), float(N * NS), AluOpType.is_lt, mul)
    V.wait_ge(S.sbs, 1)
    V.tensor_scalar(T.selk[:, :], T.selb[0:16, 0:8], float(N * NS // 512), None, mul).then_inc(S.sks, 1)
    V.wait_ge(S.sks, 1)
    for q in both:
        term(T.ofl, float(q), T.selk[:, q:q + 1], AluOpType.is_equal, mul)
    V.wait_ge(S.fs0, len(terms) - 1)
    lvl = 1
    while len(terms) > 1:
        new = []
        for i in range(0, len(terms) - 1, 2):
            o = T["f%d" % nf[0]]
            nf[0] += 1
            V.tensor_tensor(o[:, :], terms[i][:, :], terms[i + 1][:, :], add).then_inc(S["fs%d" % lvl], 1)
            new.append(o)
        V.wait_ge(S["fs%d" % lvl], len(new))
        terms = new + terms[2 * len(new):]
        lvl += 1
    V.tensor_copy(T.pu[:, :], terms[0][:, :]).then_inc(S.fs4, 1)
    Y.wait_ge(S.fs4, 1)
    for k in range(8):
        Y.dma_start(T.poff[16 * k:16 * k + 16, :], T.pu[:, :]).then_inc(S.pr, 16)

    V.wait_ge(S.wl, 32)
    V.quantize_mx(T.w_c[:, :], T.w_s[:, :], T.ws[:, :]).then_inc(S.wq, 1)
    g.wait_ge(S.wq, 1)
    chip_write(rel, T.xr_c[:, :].bitcast(U8), T.w_c[:, :].bitcast(U8), S.rec)
    chip_write(rel, T.xr_s[:, :], T.w_s[:, :], S.res)

    V.wait_ge(S.sos, 1)
    A.wait_ge(S.sos, 1)
    V.wait_ge(S.xl, 16)
    A.wait_ge(S.xl, 16)

    def tokens(k, nv):
        tile = T["tk%d" % k]
        if k:
            q = groups[(ci + k) % C][0]
            runs = [(0, 768, 6 * q, 6 * q + 12)]
        else:
            runs = [(384 * b, 384 * b + 384, 6 * q, 6 * q + 6) for b, q in enumerate([r, mate] if mine else [mate, r])]
        for t in range(4):
            for c0, c1, l0, l1 in runs:
                win = T.xs[:, t:4 * TK].indirect(T.soff[:, l0:l1])
                if t < nv:
                    V.tensor_copy(tile[:, c0 + t:c1:4], win).then_inc(S["vg%d" % k], 1)
                else:
                    A.activation(tile[:, c0 + t:c1:4], win, Copy).then_inc(S["sg%d" % k], 1)
        if nv:
            V.wait_ge(S["vg%d" % k], nv * len(runs))
        V.wait_ge(S["sg%d" % k], (4 - nv) * len(runs))
        qc, qs, c = (T["q%d_c" % k], T["q%d_s" % k], 0) if k else (T.r_c, T.r_s, 3 * CAPP * mine)
        V.quantize_mx(qc[:, c:c + 192], qs[:, c:c + 192], tile[:, :]).then_inc(S["tq%d" % k], 1)
        g.wait_ge(S["tq%d" % k], 1)
        if k == 0:
            c, h = 4 * CAPP * mine, _slot_col(groups, mate, r)
            chip_write(cores[mate], T.r_c[:, h:h + 96].bitcast(U8), T.r_c[:, c:c + 96].bitcast(U8), S.tokM)
            chip_write(cores[mate], T.r_s[:, h:h + 96], T.r_s[:, c:c + 96], S.tokM)
            return
        to = [(d, _slot_col(groups, d, r), 96 * b) for b, d in enumerate(groups[(ci + k) % C])]
        sem = S["tok%d" % k]
        _pair(g, T, topo, sent, eng, [(d, T.r_c[:, h:h + 96].bitcast(U8), qc[:, b:b + 96].bitcast(U8), sem) for d, h, b in to])
        _pair(g, T, topo, sent, eng, [(d, T.r_s[:, h:h + 96], qs[:, b:b + 96], sem) for d, h, b in to])

    tokens(TORD[0], 2)
    chip_write(cores[mate], T.m_c[:, :].bitcast(U8), T.w_c[:, :].bitcast(U8), S.me)
    chip_write(cores[mate], T.m_s[:, :], T.w_s[:, :], S.me)
    tokens(TORD[1], 2)
    tokens(TORD[2], 2)

    V.wait_ge(S.sela, per * len(wants))
    V.wait_ge(S.lns, 1)
    for k in EORD:
        for b in range(2):
            j = 2 * (k - 2) + b
            V.tensor_scalar(T["eo%d" % k][:, 32 * b:32 * b + 32], T.lin[:, :], T.sland[:, j:j + 1], 0.0,
                            add, AluOpType.max).then_inc(S["eos%d" % k], 1)
    tokens(0, 0)
    A.wait_ge(S.wl, 32)
    for k in EORD:
        eo, et = T["eo%d" % k], T["et%d" % k]
        xc, xp = T["x%d_c" % k], T["x%d_s" % k]
        V.wait_ge(S["eos%d" % k], 2)
        A.wait_ge(S["eos%d" % k], 2)
        A.activation(et[:, 0:16 * SP], T.ws[:, :].indirect(eo[:, 0:SP]), Copy).then_inc(S["sge%d" % k], 1)
        V.tensor_copy(et[:, 16 * SP:1024], T.ws[:, :].indirect(eo[:, SP:64])).then_inc(S["vge%d" % k], 1)
        V.wait_ge(S["vge%d" % k], 1)
        V.wait_ge(S["sge%d" % k], 1)
        V.quantize_mx(xc[:, :], xp[:, :], et[:, :]).then_inc(S["eq%d" % k], 1)
        g.wait_ge(S["eq%d" % k], 1)
        chip_write(rel, xc[:, 128:256].bitcast(U8), xc[:, 128:256].bitcast(U8), S["rec%d" % k])
        chip_write(rel, xp[:, 128:256], xp[:, 128:256], S["res%d" % k])
        _chosen(g, r, k, 0, False, groups, T, topo, sent, eng)
        _chosen(g, r, k, 0, True, groups, T, topo, sent, eng)

    g.wait_ge(S.un, 2 * len(eng))
    chip_write(cores[mate], T.u_c[:, 256:512].bitcast(U8), T.u_c[:, 0:256].bitcast(U8), S.us)
    chip_write(cores[mate], T.u_s[:, 256:512], T.u_s[:, 0:256], S.us)

    blocks = [(block(r), T.w_c, T.w_s, 0, S.wq, 1), (block(r, 1), T.w_c, T.w_s, 128, None, 0),
              (block(mate), T.m_c, T.m_s, 0, S.me, 2 * len(ups)), (block(mate, 1), T.m_c, T.m_s, 128, None, 0)]

    def chosen(k):
        for q in groups[(ci - k) % C]:
            j = oth.index(q)
            blocks.append((block(q), T.e_c, T.e_s, 128 * j, S["ex%d" % j], 2 * len(eng)))

    for i, q in enumerate(prev):
        blocks.append((block(q, mine), T.u_c, T.u_s, 128 * i, S.un, 2 * len(eng)))
    chosen(EORD[0])
    for i, q in enumerate(prev):
        blocks.append((block(q, 1 - mine), T.u_c, T.u_s, 256 + 128 * i, S.us, 2 * len(ups)))
    chosen(EORD[1])

    half_chips = [[(_base(groups, r) + 2 * hf + j) % C for j in range(2)] for hf in range(2)]
    h0 = [hf for hf in range(2) if (ci - TORD[-1]) % C not in half_chips[hf]][0]
    units = ([(i, h0) for i in range(4)] + [(i, 1 - h0) for i in range(4)]
             + [(i, hf) for i in range(4, len(blocks)) for hf in (h0, 1 - h0)])
    waited = set()

    def once(sem, cnt):
        if sem is not None and sem not in waited:
            waited.add(sem)
            Te.wait_ge(sem, cnt)

    for u, (i, hf) in enumerate(units):
        blk, wc, wsc, col, sem, cnt = blocks[i]
        once(sem, cnt)
        for c in half_chips[hf]:
            if c == ci:
                once(S.tq0, 1)
                once(S.tokM, 2 * len(ups))
            else:
                once(S["tok%d" % ((ci - c) % C)], 2 * len(eng))
        if u >= 8:
            Te.wait_ge(S["ev%d" % (u - 8)], 1)
        b0, c0, p0 = 512 * (u % 8), _half_col(groups, r, hf), NS * blk + HALF * hf
        Te.matmul_mx(T.ps[:, b0:b0 + HALF], wc[:, col:col + 128], wsc[:, col:col + 128],
                     T.r_c[:, c0:c0 + HALF], T.r_s[:, c0:c0 + HALF], True, True).then_inc(S["mm%d" % u], 1)
        ev = S["ev%d" % u] if u < len(units) - 8 else S.evz
        if u % 2 == 0:
            V.wait_ge(S["mm%d" % u], 1)
            V.tensor_copy(T.pw[:, p0:p0 + HALF], T.ps[:, b0:b0 + HALF]).then_inc(ev, 1)
        else:
            A.wait_ge(S["mm%d" % u], 1)
            A.activation(T.pw[:, p0:p0 + HALF], T.ps[:, b0:b0 + HALF], Copy).then_inc(ev, 1)

    for E in (V, A):
        E.wait_ge(S.pr, 128)
        E.wait_ge(S.evz, 8)
    V.tensor_copy(T.yb[:, 0:256], T.pw[:, :].indirect(T.poff[:, 0:16])).then_inc(S.yg, 1)
    A.activation(T.yb[:, 256:512], T.pw[:, :].indirect(T.poff[:, 16:32]), Copy).then_inc(S.yh, 1)
    Y.wait_ge(S.yg, 1)
    Y.dma_start(T.y[:, 0:256], T.yb[:, 0:256]).then_inc(S.y0, 16)
    A.wait_ge(S.yh, 1)
    A.dma_start(T.y[:, 256:512], T.yb[:, 256:512]).then_inc(S.y1, 16)
    Y.wait_ge(S.y0, 16)
    A.wait_ge(S.y1, 16)
    g.wait_ge(S.sent, sent[0])
